import numpy as np
import ml_dtypes


def mxq(x, axis, fmt="e4m3"):
    dtype, down = {"e4m3": (ml_dtypes.float8_e4m3fn, 7), "e5m2": (ml_dtypes.float8_e5m2, 14)}[fmt]
    v = np.moveaxis(np.asarray(x, np.float32).astype(ml_dtypes.bfloat16).astype(np.float64), axis, -1)
    blocks = v.reshape(v.shape[:-1] + (-1, 32))
    amax = np.abs(blocks).max(-1, keepdims=True)
    byte = np.maximum(np.where(amax > 0, np.frexp(amax)[1] - 1 + 127, 0) - down, 1)
    scale = np.exp2(byte - 127.0)
    codes = (blocks / scale).astype(np.float32).astype(dtype).astype(np.float64)
    return np.moveaxis((codes * scale).reshape(v.shape), -1, axis)


WIDE = False


def mx_kscale(k):
    if not WIDE:
        return np.ones(k)
    levels = np.array([10, -10, 5, -5, 0])
    if k % 512:
        return np.exp2(np.random.permutation(np.resize(levels, k // 32))).repeat(32)
    a = np.empty((k // 512, 16))
    for p in range(k // 512):
        a[p, :8] = np.random.permutation(np.resize(levels, 8))
        for g in range(8):
            far = levels[np.abs(levels - a[p, g]) >= 10]
            a[p, g + 8] = far[np.random.randint(len(far))]
    return np.exp2(a.ravel()).repeat(32)


def f64(x):
    return np.asarray(x).astype(np.float64)


def striped(idx):
    return np.tile(idx.reshape(-1, 16).T, (8, 1)).astype(np.uint16)


def unstriped(offs):
    return offs[:16].T.reshape(-1).astype(np.int64)


E2M1 = np.array([0.0, 0.5, 1.0, 1.5, 2.0, 3.0, 4.0, 6.0, -0.0, -0.5, -1.0, -1.5, -2.0, -3.0, -4.0, -6.0])


def pack_weight(w, fmt):
    k, n = w.shape
    w = f64(np.asarray(w, np.float32).astype(ml_dtypes.bfloat16)).reshape(k // 32, 32, n)
    amax = np.abs(w).max(1)
    if fmt == "e4m3":
        byte = np.frexp(amax)[1] - 1 + 127 - 7
    else:
        mant, ex = np.frexp(amax / 6.0)
        byte = np.where(mant > 0.5, ex, ex - 1) + 127
    byte = np.clip(np.where(amax > 0, byte, 1), 1, 254)
    scaled = (w * np.exp2(127.0 - byte)[:, None, :]).reshape(k, n).astype(np.float32)
    by_word = np.ascontiguousarray(scaled.reshape(k // 512, 128, 4, n).transpose(0, 1, 3, 2))
    if fmt == "e4m3":
        words = by_word.astype(ml_dtypes.float8_e4m3fn).view(np.uint8)
    else:
        c = by_word.astype(ml_dtypes.float4_e2m1fn).view(np.uint8) & 0xF
        words = (c[..., 0::2] | (c[..., 1::2] << 4)).reshape(k // 512, 128, 2 * n)
    return np.ascontiguousarray(words), np.ascontiguousarray(byte.astype(np.uint8).reshape(k // 512, 16, n))


def unpack_weight(words, scales, fmt):
    g, _, n = scales.shape
    words = np.ascontiguousarray(words).reshape(g, 128, n, -1)
    if fmt == "e4m3":
        vals = words.view(ml_dtypes.float8_e4m3fn).astype(np.float64)
    else:
        nib = np.empty((g, 128, n, 4), np.uint8)
        nib[..., 0::2] = words & 0xF
        nib[..., 1::2] = words >> 4
        vals = E2M1[nib]
    vals = vals * np.repeat(np.exp2(scales.astype(np.float64) - 127.0), 8, axis=1)[..., None]
    return vals.transpose(0, 1, 3, 2).reshape(g * 512, n)


def gelu(v):
    return 0.5 * v * (1.0 + np.tanh(np.sqrt(2.0 / np.pi) * (v + 0.044715 * v**3)))


def bf(x):
    return np.asarray(x, np.float32).astype(ml_dtypes.bfloat16)

def planes(Y):
    n, m = Y.shape
    b = f64(bf(Y)).reshape(n // 32, 32, m)
    amax = np.abs(b).max(1)
    byte = np.clip(np.where(amax > 0, np.frexp(amax)[1] - 1 + 127 - 7, 1), 1, 254)
    codes = (b * np.exp2(127.0 - byte)[:, None, :]).reshape(n, m).astype(np.float32).astype(ml_dtypes.float8_e4m3fn).view(np.uint8)
    words = codes.reshape(n // 512, 128, 4, m).transpose(0, 1, 3, 2)
    return np.ascontiguousarray(words), np.ascontiguousarray(byte.astype(np.uint8).reshape(n // 512, 16, m))


K, C, R, N, T, S, T2 = 1024, 512, 1024, 512, 2048, 1024, 2048

def setup_inputs():
    n = np.random.standard_normal
    s = mx_kscale(K)[:, None]
    u = mx_kscale(R)[:, None]
    phi = 2 * np.pi * np.random.random((C, T))
    theta = 2 * np.pi * np.random.random((C, R))
    amp = np.sqrt(2 / C)
    tab_words, tab_scales = pack_weight(np.concatenate([np.cos(phi), np.sin(phi)], 0) * s, "e4m3")
    wd_words, wd_scales = pack_weight(n((R, N)) / np.sqrt(R) / u, "e2m1")
    return {
        "tab_words": tab_words, "tab_scales": tab_scales,
        "offs": striped(np.random.permutation(T)[:S]),
        "pc": (amp * np.cos(theta) / s[:C] * u.T).astype(np.float32),
        "ps": (amp * np.sin(theta) / s[C:] * u.T).astype(np.float32),
        "ref": (0.5 * n(R) * u[:, 0]).astype(np.float32),
        "wd_words": wd_words, "wd_scales": wd_scales,
        "gain": np.exp(0.8 * n(N)).astype(np.float32),
        "wgo": np.exp(0.3 * n((128, S))).astype(np.float32),
        "offs2": striped(np.random.permutation(T2)[:S]),
    }

def reference(tab_words, tab_scales, offs, pc, ps, ref, wd_words, wd_scales, gain, wgo, offs2):
    v = unpack_weight(tab_words, tab_scales, "e4m3")[:, unstriped(offs)]
    fc = mxq(f64(pc), 0, "e4m3").T @ v[:C]
    fs = mxq(f64(ps), 0, "e4m3").T @ v[C:]
    h = fc - fs + f64(ref)[:, None]
    wd = unpack_weight(wd_words, wd_scales, "e2m1")
    z = wd.T @ mxq(h, 0, "e4m3")
    y = f64(gain)[:, None] * np.tanh(z)
    page = np.zeros((N, T2))
    page[:, unstriped(offs2)] = np.tile(f64(wgo), (N // 128, 1)) * y
    y = page
    words, scales = planes(y)
    return y, words, scales

@@ -1,0 +1,314 @@
+from contextlib import ExitStack
+
+import concourse.mybir as mybir
+
+K, C, R, N, T, S, T2 = 1024, 512, 1024, 512, 2048, 1024, 2048
+FLOPS = 2 * K * R * S + 2 * R * N * S
+
+F32 = mybir.dt.float32
+BF16 = mybir.dt.bfloat16
+I32 = mybir.dt.int32
+U32 = mybir.dt.uint32
+U16 = mybir.dt.uint16
+U8 = mybir.dt.uint8
+FP8X4 = mybir.dt.float8_e4m3fn_x4
+FP4X4 = mybir.dt.float4_e2m1fn_x4
+ACT = mybir.ActivationFunctionType
+ALU = mybir.AluOpType
+
+P = 128
+PACK = 4
+BLK = 512
+CH = 256
+NCH = S // CH
+HALF = 128
+TAIL = [256, 512, 512, 512, 256]
+
+
+def tile_list_hologram_detector_page_kernel(
+    tc, tab_words, tab_scales, offs, pc, ps, ref, wd_words, wd_scales, gain, wgo, offs2, out_0, out_1, out_2
+):
+    nc = tc.nc
+    with ExitStack() as ctx:
+        keep = ctx.enter_context(tc.tile_pool(name="keep", bufs=1))
+        ring = ctx.enter_context(tc.tile_pool(name="ring", bufs=3))
+        hbank = ctx.enter_context(tc.psum_pool(name="hbank", bufs=6))
+        zbank = ctx.enter_context(tc.psum_pool(name="zbank", bufs=2))
+
+        idx = keep.tile([P, S // 16], U16, name="idx")
+        idx2 = keep.tile([P, S // 16], U16, name="idx2")
+        nc.sync.dma_start(idx[:], offs)
+
+        tsc = keep.tile([P, T], U8, name="tsc", align_bytes=64)
+        wsc_raw = keep.tile([P, 2, N], U8, name="wsc_raw", align_bytes=64)
+        nc.gpsimd.memset(tsc[:].bitcast(I32), 0)
+        nc.gpsimd.memset(wsc_raw[:].bitcast(I32), 0)
+
+        warm = keep.tile([P, 8], F32, name="warm")
+        nc.vector.memset(warm[:, 0:1], 0.0)
+        nc.scalar.activation(warm[:, 1:2], warm[:, 0:1], ACT.Tanh)
+
+        def load_cols(src, c0, width, name, tag):
+            raw = keep.tile([P, PACK, width], F32, name=name, tag=tag)
+            nc.sync.dma_start(raw[:], src.rearrange("(p i) r -> p i r", i=PACK)[:, :, c0 : c0 + width])
+            return raw
+
+        def load_table(a):
+            t_a = keep.tile([P, T], U32, name="tw%d" % a, align_bytes=64)
+            nc.sync.dma_start(t_a[:].bitcast(I32), tab_words[a].rearrange("p n t -> p (n t)").bitcast(I32))
+            return t_a
+
+        ref_sb = keep.tile([P, 2, PACK], F32, name="ref_sb")
+        gain_sb = keep.tile([P, PACK], F32, name="gain_sb")
+        wd_raw = keep.tile([P, 2, 2 * N], U8, name="wd_raw", align_bytes=64)
+        nc.sync.dma_start(idx2[:], offs2)
+        nc.sync.dma_start(ref_sb[:], ref.rearrange("(b p t) -> p b t", b=2, t=PACK))
+        nc.sync.dma_start(gain_sb[:], gain.rearrange("(p t) -> p t", t=PACK))
+        for a in range(2):
+            nc.sync.dma_start(wd_raw[:, a, :].bitcast(I32), wd_words[a].bitcast(I32))
+        pc_a0 = load_cols(pc, 0, CH, "pc_a0", "pc_a0")
+        pc_a1 = load_cols(pc, CH, CH, "pc_a1", "pc_a1")
+        for q in range(4):
+            nc.sync.dma_start(tsc[32 * q : 32 * q + 8, :].bitcast(I32), tab_scales[:, 4 * q : 4 * q + 4, :].bitcast(I32))
+        tw = [load_table(0)]
+        ps_a0 = load_cols(ps, 0, CH, "ps_a0", "ps_a0")
+        ps_a1 = load_cols(ps, CH, CH, "ps_a1", "ps_a1")
+        pc_b0 = load_cols(pc, 2 * CH, CH, "pc_b0", "pc_b0")
+        tw.append(load_table(1))
+        for q in range(4):
+            nc.sync.dma_start(
+                wsc_raw[32 * q : 32 * q + 4, :, :].bitcast(I32),
+                wd_scales[:, 4 * q : 4 * q + 4, :].rearrange("a r n -> r a n").bitcast(I32),
+            )
+        pc_b1 = load_cols(pc, 3 * CH, CH, "pc_b1", "pc_b1")
+        ps_b0 = load_cols(ps, 2 * CH, CH, "ps_b0", "ps_b0_page2")
+        ps_b1 = load_cols(ps, 3 * CH, CH, "ps_b1", "ps_b1_page3")
+
+        wgo_rows = wgo.rearrange("(q t) j -> q t j", t=PACK)
+        wgo_parts = []
+        for j0, width in ((0, CH), (CH, CH), (2 * CH, 2 * CH)):
+            part = keep.tile([P, PACK, width], F32, name="wgo%d" % j0)
+            for q in (0, 2, 1, 3):
+                nc.sync.dma_start(part[32 * q : 32 * q + 32, :, :], wgo_rows[:, :, j0 : j0 + width])
+            wgo_parts.append((j0, width, part))
+
+        pages = []
+        for t in range(2):
+            page = keep.tile([P, T2], F32, name="page%d" % t)
+            for h in range(2):
+                nc.vector.memset(page[:, h * 1024 : (h + 1) * 1024], 0.0)
+            pages.append(page)
+
+        gs = keep.tile([P, S], U8, name="gs", align_bytes=64)
+        gw = []
+        for a in range(2):
+            g_a = keep.tile([P, S], U32, name="gw%d" % a, align_bytes=64)
+            gw.append(g_a)
+
+        def deal(engine, grouped, raw, c0, m0, negate):
+            dst = grouped[:, :, m0 : m0 + 64, :].rearrange("p t m i -> p m i t")
+            src = raw[:, :, c0 : c0 + 256].rearrange("p i (m t) -> p m i t", t=PACK)
+            if engine == "scalar":
+                nc.scalar.activation(dst, src, ACT.Copy, scale=-1.0 if negate else 1.0)
+            elif negate:
+                nc.vector.tensor_scalar(dst, src, -1.0, None, ALU.mult)
+            else:
+                nc.vector.tensor_copy(dst, src)
+
+        def quantise(src, width, name, pool, tag):
+            codes = pool.tile([P, width], U32, name=name + "_codes", tag=tag + "_codes", align_bytes=64)
+            scales = pool.tile([P, width], U8, name=name + "_scales", tag=tag + "_scales", align_bytes=64)
+            nc.vector.quantize_mx(out=codes[:].bitcast(FP8X4), scales=scales[:], in_=src)
+            return codes, scales
+
+        def new_grouped(name):
+            return keep.tile([P, PACK, P, PACK], BF16, name=name, align_bytes=64)
+
+        def flat(grouped):
+            return grouped[:].rearrange("p t m i -> p (t m i)")
+
+        wd = keep.tile([P, 2, PACK, P, 2], U8, name="wd", align_bytes=64)
+        wsc = keep.tile([P, 2, PACK, P], U8, name="wsc", align_bytes=64)
+        for a in range(2):
+            nc.vector.tensor_copy(
+                wd[:, a].rearrange("p t m e -> p m t e"), wd_raw[:, a, :].rearrange("p (m t e) -> p m t e", t=PACK, e=2)
+            )
+
+        prop = {}
+        g = new_grouped("g_pc_a")
+        deal("scalar", g, pc_a0, 0, 0, False)
+        deal("scalar", g, pc_a1, 0, 64, False)
+        nc.vector.tensor_copy(gs[:], tsc[:].indirect(idx[:]))
+        nc.vector.tensor_copy(gw[0][:], tw[0][:].indirect(idx[:]))
+        prop[0, 0] = quantise(flat(g), BLK, "pc_a", keep, "pc_a")
+        g = new_grouped("g_ps_a")
+        deal("scalar", g, ps_a0, 0, 0, True)
+        deal("scalar", g, ps_a1, 0, 64, True)
+        prop[1, 0] = quantise(flat(g), BLK, "ps_a", keep, "ps_a")
+        nc.vector.tensor_copy(gw[1][:, 0:CH], tw[1][:].indirect(idx[:, 0 : CH // 16]))
+        nc.vector.tensor_copy(gw[1][:, CH:S], tw[1][:].indirect(idx[:, CH // 16 : S // 16]))
+        g = new_grouped("g_pc_b")
+        deal("scalar", g, pc_b0, 0, 0, False)
+        deal("scalar", g, pc_b1, 0, 64, False)
+        prop[0, 1] = quantise(flat(g), BLK, "pc_b", keep, "pc_b")
+        g = new_grouped("g_ps_b")
+        deal("scalar", g, ps_b0, 0, 0, True)
+        deal("vector", g, ps_b1, 0, 64, True)
+        prop[1, 1] = quantise(flat(g), BLK, "ps_b", keep, "ps_b")
+        nc.vector.tensor_copy(wsc[:].rearrange("p a t m -> p a m t"), wsc_raw[:].rearrange("p a (m t) -> p a m t", t=PACK))
+
+        for t, tag in ((2, "ps_b0_page2"), (3, "ps_b1_page3")):
+            page = keep.tile([P, T2], F32, name="page%d" % t, tag=tag)
+            for h in range(8):
+                nc.gpsimd.memset(page[:, h * 256 : (h + 1) * 256], 0.0)
+            pages.append(page)
+
+        def field_pass(out, a, b, t, j0, width, start, stop):
+            codes, scales = prop[a, b]
+            nc.tensor.matmul_mx(
+                out=out,
+                lhsT=codes[:, t * P : (t + 1) * P].bitcast(FP8X4),
+                lhsT_scale=scales[:, t * P : (t + 1) * P],
+                rhs=gw[a][:, j0 : j0 + width].bitcast(FP8X4),
+                rhs_scale=gs[4 * a : P, j0 : j0 + width],
+                start=start,
+                stop=stop,
+            )
+
+        hq = {}
+
+        def field_first(b):
+            banks = []
+            for jh in range(2):
+                bank = hbank.tile([P, PACK, HALF], F32, name="hb", tag="hb")
+                banks.append(bank)
+            for a in range(2):
+                for jh in range(2):
+                    for t in range(PACK):
+                        field_pass(banks[jh][:, t, :], a, b, t, jh * HALF, HALF, a == 0 and t == 0, a == 1 and t == PACK - 1)
+            hg = []
+            for jh in range(2):
+                hgj = keep.tile([P, HALF, PACK], BF16, name="hg0_%d_%d" % (b, jh), align_bytes=64)
+                nc.vector.tensor_tensor(
+                    hgj[:],
+                    banks[jh][:].rearrange("p t j -> p j t"),
+                    ref_sb[:, b : b + 1, :].to_broadcast([P, HALF, PACK]),
+                    ALU.add,
+                )
+                hg.append(hgj)
+            for jh in range(2):
+                name = "h0_%d_%d" % (b, jh)
+                codes, scales = quantise(hg[jh][:].rearrange("p j t -> p (j t)"), HALF, name, keep, name)
+                hq[0, b, jh] = (codes[:], scales[:])
+
+        def field(c, b):
+            planes = ring.tile([P, PACK, CH], BF16, name="hplanes", tag="hplanes")
+            for u in range(2):
+                bank = hbank.tile([P, 2, CH], F32, name="hb", tag="hb")
+                for e in range(2):
+                    for a in range(2):
+                        field_pass(bank[:, e, :], a, b, 2 * u + e, c * CH, CH, a == 0, a == 1)
+                for e in range(2):
+                    t = 2 * u + e
+                    nc.scalar.activation(planes[:, t, :], bank[:, e, :], ACT.Identity, bias=ref_sb[:, b, t : t + 1])
+            hg = ring.tile([P, CH, PACK], BF16, name="hg", tag="hg", align_bytes=64)
+            nc.scalar.copy(
+                hg[:].rearrange("p (c i) t -> p c t i", i=4), planes[:].rearrange("p t (c i) -> p c t i", i=4)
+            )
+            name = "h%d_%d" % (c, b)
+            codes, scales = quantise(hg[:].rearrange("p j t -> p (j t)"), CH, name, keep, name)
+            for jh in range(2):
+                hq[c, b, jh] = (codes[:, jh * HALF : (jh + 1) * HALF], scales[:, jh * HALF : (jh + 1) * HALF])
+
+        ys = [keep.tile([P, S], F32, name="y%d" % t) for t in range(PACK)]
+
+        def detect(t, c):
+            bank = zbank.tile([P, CH], F32, name="zb", tag="zb")
+            for jh in range(2):
+                for a in range(2):
+                    codes, scales = hq[c, a, jh]
+                    nc.tensor.matmul_mx(
+                        out=bank[:, jh * HALF : (jh + 1) * HALF],
+                        lhsT=wd[:, a, t].rearrange("p m e -> p (m e)").bitcast(FP4X4),
+                        lhsT_scale=wsc[:, a, t, :],
+                        rhs=codes.bitcast(FP8X4),
+                        rhs_scale=scales,
+                        start=(a == 0),
+                        stop=(a == 1),
+                    )
+            nc.scalar.activation(ys[t][:, c * CH : (c + 1) * CH], bank[:], ACT.Tanh)
+
+        def scatter(t, c0, c1):
+            j0, j1 = c0 * CH, c1 * CH
+            wg = ring.tile([P, j1 - j0], F32, name="wg", tag="wg")
+            for p0, width, part in wgo_parts:
+                lo, hi = max(j0, p0), min(j1, p0 + width)
+                if lo < hi:
+                    nc.vector.tensor_scalar(
+                        wg[:, lo - j0 : hi - j0], part[:, t, lo - p0 : hi - p0], gain_sb[:, t : t + 1], None, ALU.mult
+                    )
+            nc.vector.tensor_tensor(
+                pages[t][:].indirect(idx2[:, j0 // 16 : j1 // 16]), ys[t][:, j0:j1], wg[:], ALU.mult
+            )
+
+        def detect_scatter(t, c):
+            detect(t, c)
+            scatter(t, c, c + 1)
+
+        out_rows = out_0.rearrange("(p t) m -> p t m", t=PACK)
+        pairs = []
+        m0 = 0
+        for n, width in enumerate(TAIL):
+            pair = keep.tile([P, 2, width, 2], BF16, name="pair%d" % n)
+            pairs.append((m0, width, pair))
+            m0 = m0 + width
+
+        def finish_page(t):
+            nc.sync.dma_start(out_rows[:, t, :], pages[t][:])
+            for m0, width, pair in pairs:
+                nc.scalar.copy(pair[:, t // 2, :, t % 2], pages[t][:, m0 : m0 + width])
+
+        field_first(0)
+        field_first(1)
+        field(1, 0)
+        detect_scatter(0, 0)
+        detect_scatter(1, 0)
+        field(1, 1)
+        detect_scatter(2, 0)
+        detect_scatter(3, 0)
+        field(2, 0)
+        detect_scatter(0, 1)
+        detect_scatter(1, 1)
+        field(2, 1)
+        detect_scatter(2, 1)
+        field(3, 0)
+        detect_scatter(0, 2)
+        detect_scatter(1, 2)
+        field(3, 1)
+        detect(2, 2)
+        detect(3, 1)
+        detect(3, 2)
+        detect_scatter(0, 3)
+        detect_scatter(1, 3)
+        detect(2, 3)
+        scatter(2, 2, 4)
+        detect(3, 3)
+        scatter(3, 1, 4)
+        for t in range(PACK):
+            finish_page(t)
+
+        yscales = keep.tile([P, T2], U8, name="yscales", align_bytes=64)
+        words_out = out_1[0].rearrange("p m t -> p (m t)")
+        for n, (m0, width, pair) in enumerate(pairs):
+            yg = keep.tile([P, width, PACK], BF16, name="yg%d" % n, align_bytes=64)
+            nc.vector.tensor_copy(
+                yg[:].rearrange("p m t -> p (m t)").bitcast(I32).rearrange("p (m u) -> p m u", u=2),
+                pair[:].rearrange("p u m e -> p u (m e)").bitcast(I32).rearrange("p u m -> p m u"),
+            )
+            ywords = keep.tile([P, width], U32, name="ywords%d" % n, align_bytes=64)
+            nc.vector.quantize_mx(
+                out=ywords[:].bitcast(FP8X4), scales=yscales[:, m0 : m0 + width], in_=yg[:].rearrange("p m t -> p (m t)")
+            )
+            nc.sync.dma_start(words_out[:, 4 * m0 : 4 * (m0 + width)].bitcast(I32), ywords[:].bitcast(I32))
+        for q in range(4):
+            nc.sync.dma_start(out_2[0, 4 * q : 4 * q + 4, :].bitcast(I32), yscales[32 * q : 32 * q + 4, :].bitcast(I32))

@@ -23,6 +23,10 @@ CH = 256
 NCH = S // CH
 HALF = 128
 TAIL = [256, 512, 512, 512, 256]
+TAIL_STYLE = "pairs"
+TAIL_SCALAR = ()
+WD16 = True
+HOLD = True
 
 
 def tile_list_hologram_detector_page_kernel(
@@ -31,15 +35,13 @@ def tile_list_hologram_detector_page_kernel(
     nc = tc.nc
     with ExitStack() as ctx:
         keep = ctx.enter_context(tc.tile_pool(name="keep", bufs=1))
-        ring = ctx.enter_context(tc.tile_pool(name="ring", bufs=3))
-        hbank = ctx.enter_context(tc.psum_pool(name="hbank", bufs=6))
-        zbank = ctx.enter_context(tc.psum_pool(name="zbank", bufs=2))
+        hbank = ctx.enter_context(tc.psum_pool(name="hbank", bufs=1))
 
         idx = keep.tile([P, S // 16], U16, name="idx")
         idx2 = keep.tile([P, S // 16], U16, name="idx2")
         nc.sync.dma_start(idx[:], offs)
 
-        tsc = keep.tile([P, T], U8, name="tsc", align_bytes=64)
+        tsc = keep.tile([P, T], U8, name="tsc", tag="pc_a_codes", align_bytes=64)
         wsc_raw = keep.tile([P, 2, N], U8, name="wsc_raw", align_bytes=64)
         nc.gpsimd.memset(tsc[:].bitcast(I32), 0)
         nc.gpsimd.memset(wsc_raw[:].bitcast(I32), 0)
@@ -49,7 +51,7 @@ def tile_list_hologram_detector_page_kernel(
         nc.scalar.activation(warm[:, 1:2], warm[:, 0:1], ACT.Tanh)
 
         def load_cols(src, c0, width, name, tag):
-            raw = keep.tile([P, PACK, width], F32, name=name, tag=tag)
+            raw = keep.tile([P, PACK, width], F32, name=name, tag=tag, align_bytes=64)
             nc.sync.dma_start(raw[:], src.rearrange("(p i) r -> p i r", i=PACK)[:, :, c0 : c0 + width])
             return raw
 
@@ -58,11 +60,12 @@ def tile_list_hologram_detector_page_kernel(
             nc.sync.dma_start(t_a[:].bitcast(I32), tab_words[a].rearrange("p n t -> p (n t)").bitcast(I32))
             return t_a
 
-        ref_sb = keep.tile([P, 2, PACK], F32, name="ref_sb")
+        ref_sb = keep.tile([P, 2, 2 * PACK], F32, name="ref_sb")
         gain_sb = keep.tile([P, PACK], F32, name="gain_sb")
         wd_raw = keep.tile([P, 2, 2 * N], U8, name="wd_raw", align_bytes=64)
         nc.sync.dma_start(idx2[:], offs2)
-        nc.sync.dma_start(ref_sb[:], ref.rearrange("(b p t) -> p b t", b=2, t=PACK))
+        for b in range(2):
+            nc.sync.dma_start(ref_sb[:, b, 0:PACK], ref[b * BLK : (b + 1) * BLK].rearrange("(p t) -> p t", t=PACK))
         nc.sync.dma_start(gain_sb[:], gain.rearrange("(p t) -> p t", t=PACK))
         for a in range(2):
             nc.sync.dma_start(wd_raw[:, a, :].bitcast(I32), wd_words[a].bitcast(I32))
@@ -71,26 +74,28 @@ def tile_list_hologram_detector_page_kernel(
         for q in range(4):
             nc.sync.dma_start(tsc[32 * q : 32 * q + 8, :].bitcast(I32), tab_scales[:, 4 * q : 4 * q + 4, :].bitcast(I32))
         tw = [load_table(0)]
-        ps_a0 = load_cols(ps, 0, CH, "ps_a0", "ps_a0")
-        ps_a1 = load_cols(ps, CH, CH, "ps_a1", "ps_a1")
-        pc_b0 = load_cols(pc, 2 * CH, CH, "pc_b0", "pc_b0")
-        tw.append(load_table(1))
         for q in range(4):
             nc.sync.dma_start(
                 wsc_raw[32 * q : 32 * q + 4, :, :].bitcast(I32),
                 wd_scales[:, 4 * q : 4 * q + 4, :].rearrange("a r n -> r a n").bitcast(I32),
             )
-        pc_b1 = load_cols(pc, 3 * CH, CH, "pc_b1", "pc_b1")
-        ps_b0 = load_cols(ps, 2 * CH, CH, "ps_b0", "ps_b0_page2")
+        ps_a = load_cols(ps, 0, BLK, "ps_a", "ps_a")
+        tw.append(load_table(1))
+        pc_b0 = load_cols(pc, 2 * CH, CH, "pc_b0", "pc_b0")
+        pc_b1 = load_cols(pc, 3 * CH, CH, "pc_b1", "pc_b1_page2")
+        ps_b0 = load_cols(ps, 2 * CH, CH, "ps_b0", "hplanes1_0")
         ps_b1 = load_cols(ps, 3 * CH, CH, "ps_b1", "ps_b1_page3")
 
         wgo_rows = wgo.rearrange("(q t) j -> q t j", t=PACK)
-        wgo_parts = []
-        for j0, width in ((0, CH), (CH, CH), (2 * CH, 2 * CH)):
-            part = keep.tile([P, PACK, width], F32, name="wgo%d" % j0)
+        wgo_first = keep.tile([P, PACK, CH], F32, name="wgo_first")
+        for q in (0, 2, 1, 3):
+            nc.sync.dma_start(wgo_first[32 * q : 32 * q + 32, :, :], wgo_rows[:, :, 0:CH])
+        wgo_rest = []
+        for u in range(2):
+            part = keep.tile([P, 2, S - CH], F32, name="wgo_rest%d" % u)
             for q in (0, 2, 1, 3):
-                nc.sync.dma_start(part[32 * q : 32 * q + 32, :, :], wgo_rows[:, :, j0 : j0 + width])
-            wgo_parts.append((j0, width, part))
+                nc.sync.dma_start(part[32 * q : 32 * q + 32, :, :], wgo_rows[:, 2 * u : 2 * u + 2, CH:S])
+            wgo_rest.append(part)
 
         pages = []
         for t in range(2):
@@ -100,10 +105,13 @@ def tile_list_hologram_detector_page_kernel(
             pages.append(page)
 
         gs = keep.tile([P, S], U8, name="gs", align_bytes=64)
-        gw = []
-        for a in range(2):
-            g_a = keep.tile([P, S], U32, name="gw%d" % a, align_bytes=64)
-            gw.append(g_a)
+        gw0 = keep.tile([P, S], U32, name="gw0", align_bytes=64)
+        gw1 = [keep.tile([P, S // 2], U32, name="gw1_0", align_bytes=64)]
+
+        def gathered(a, j0, width):
+            if a == 0:
+                return gw0[:, j0 : j0 + width]
+            return gw1[j0 // 512][:, j0 % 512 : j0 % 512 + width]
 
         def deal(engine, grouped, raw, c0, m0, negate):
             dst = grouped[:, :, m0 : m0 + 64, :].rearrange("p t m i -> p m i t")
@@ -130,23 +138,28 @@ def tile_list_hologram_detector_page_kernel(
         wd = keep.tile([P, 2, PACK, P, 2], U8, name="wd", align_bytes=64)
         wsc = keep.tile([P, 2, PACK, P], U8, name="wsc", align_bytes=64)
         for a in range(2):
-            nc.vector.tensor_copy(
-                wd[:, a].rearrange("p t m e -> p m t e"), wd_raw[:, a, :].rearrange("p (m t e) -> p m t e", t=PACK, e=2)
-            )
+            if WD16:
+                nc.vector.tensor_copy(
+                    wd[:, a].rearrange("p t m e -> p (t m e)").bitcast(U16).rearrange("p (t m) -> p m t", t=PACK),
+                    wd_raw[:, a, :].bitcast(U16).rearrange("p (m t) -> p m t", t=PACK),
+                )
+            else:
+                nc.vector.tensor_copy(
+                    wd[:, a].rearrange("p t m e -> p m t e"), wd_raw[:, a, :].rearrange("p (m t e) -> p m t e", t=PACK, e=2)
+                )
 
         prop = {}
         g = new_grouped("g_pc_a")
         deal("scalar", g, pc_a0, 0, 0, False)
         deal("scalar", g, pc_a1, 0, 64, False)
         nc.vector.tensor_copy(gs[:], tsc[:].indirect(idx[:]))
-        nc.vector.tensor_copy(gw[0][:], tw[0][:].indirect(idx[:]))
+        nc.vector.tensor_copy(gw0[:], tw[0][:].indirect(idx[:]))
         prop[0, 0] = quantise(flat(g), BLK, "pc_a", keep, "pc_a")
         g = new_grouped("g_ps_a")
-        deal("scalar", g, ps_a0, 0, 0, True)
-        deal("scalar", g, ps_a1, 0, 64, True)
+        deal("scalar", g, ps_a, 0, 0, True)
+        deal("scalar", g, ps_a, CH, 64, True)
         prop[1, 0] = quantise(flat(g), BLK, "ps_a", keep, "ps_a")
-        nc.vector.tensor_copy(gw[1][:, 0:CH], tw[1][:].indirect(idx[:, 0 : CH // 16]))
-        nc.vector.tensor_copy(gw[1][:, CH:S], tw[1][:].indirect(idx[:, CH // 16 : S // 16]))
+        nc.vector.tensor_copy(gw1[0][:], tw[1][:].indirect(idx[:, 0:32]))
         g = new_grouped("g_pc_b")
         deal("scalar", g, pc_b0, 0, 0, False)
         deal("scalar", g, pc_b1, 0, 64, False)
@@ -157,8 +170,8 @@ def tile_list_hologram_detector_page_kernel(
         prop[1, 1] = quantise(flat(g), BLK, "ps_b", keep, "ps_b")
         nc.vector.tensor_copy(wsc[:].rearrange("p a t m -> p a m t"), wsc_raw[:].rearrange("p a (m t) -> p a m t", t=PACK))
 
-        for t, tag in ((2, "ps_b0_page2"), (3, "ps_b1_page3")):
-            page = keep.tile([P, T2], F32, name="page%d" % t, tag=tag)
+        for t, tag in ((2, "pc_b1_page2"), (3, "ps_b1_page3")):
+            page = keep.tile([P, T2], F32, name="page%d" % t, tag=tag, align_bytes=64)
             for h in range(8):
                 nc.gpsimd.memset(page[:, h * 256 : (h + 1) * 256], 0.0)
             pages.append(page)
@@ -169,7 +182,7 @@ def tile_list_hologram_detector_page_kernel(
                 out=out,
                 lhsT=codes[:, t * P : (t + 1) * P].bitcast(FP8X4),
                 lhsT_scale=scales[:, t * P : (t + 1) * P],
-                rhs=gw[a][:, j0 : j0 + width].bitcast(FP8X4),
+                rhs=gathered(a, j0, width).bitcast(FP8X4),
                 rhs_scale=gs[4 * a : P, j0 : j0 + width],
                 start=start,
                 stop=stop,
@@ -180,7 +193,7 @@ def tile_list_hologram_detector_page_kernel(
         def field_first(b):
             banks = []
             for jh in range(2):
-                bank = hbank.tile([P, PACK, HALF], F32, name="hb", tag="hb")
+                bank = hbank.tile([P, PACK, HALF], F32, name="hb", tag="hb%d_%d" % (b, jh))
                 banks.append(bank)
             for a in range(2):
                 for jh in range(2):
@@ -188,11 +201,11 @@ def tile_list_hologram_detector_page_kernel(
                         field_pass(banks[jh][:, t, :], a, b, t, jh * HALF, HALF, a == 0 and t == 0, a == 1 and t == PACK - 1)
             hg = []
             for jh in range(2):
-                hgj = keep.tile([P, HALF, PACK], BF16, name="hg0_%d_%d" % (b, jh), align_bytes=64)
+                hgj = keep.tile([P, HALF, PACK], BF16, name="hg0_%d_%d" % (b, jh), tag="hg0_%d_%d" % (b, jh), align_bytes=64)
                 nc.vector.tensor_tensor(
                     hgj[:],
                     banks[jh][:].rearrange("p t j -> p j t"),
-                    ref_sb[:, b : b + 1, :].to_broadcast([P, HALF, PACK]),
+                    ref_sb[:, b : b + 1, 0:PACK].to_broadcast([P, HALF, PACK]),
                     ALU.add,
                 )
                 hg.append(hgj)
@@ -201,29 +214,37 @@ def tile_list_hologram_detector_page_kernel(
                 codes, scales = quantise(hg[jh][:].rearrange("p j t -> p (j t)"), HALF, name, keep, name)
                 hq[0, b, jh] = (codes[:], scales[:])
 
-        def field(c, b):
-            planes = ring.tile([P, PACK, CH], BF16, name="hplanes", tag="hplanes")
+        def field(c, b, t_rest=None):
+            planes = keep.tile([P, PACK, CH], BF16, name="hplanes", tag="hplanes%d_%d" % (c, b), align_bytes=64)
             for u in range(2):
-                bank = hbank.tile([P, 2, CH], F32, name="hb", tag="hb")
+                bank = hbank.tile([P, 2, CH], F32, name="hb", tag="hb%d_%d" % ((2 * c + b) % 3, u))
                 for e in range(2):
                     for a in range(2):
                         field_pass(bank[:, e, :], a, b, 2 * u + e, c * CH, CH, a == 0, a == 1)
                 for e in range(2):
                     t = 2 * u + e
                     nc.scalar.activation(planes[:, t, :], bank[:, e, :], ACT.Identity, bias=ref_sb[:, b, t : t + 1])
-            hg = ring.tile([P, CH, PACK], BF16, name="hg", tag="hg", align_bytes=64)
+            hg = keep.tile([P, CH, PACK], BF16, name="hg", tag="hg%d_%d" % (c % 2, b), align_bytes=64)
             nc.scalar.copy(
                 hg[:].rearrange("p (c i) t -> p c t i", i=4), planes[:].rearrange("p t (c i) -> p c t i", i=4)
             )
+            if t_rest is not None:
+                weights_rest(t_rest, "hplanes%d_%d" % (c, b))
             name = "h%d_%d" % (c, b)
             codes, scales = quantise(hg[:].rearrange("p j t -> p (j t)"), CH, name, keep, name)
             for jh in range(2):
                 hq[c, b, jh] = (codes[:, jh * HALF : (jh + 1) * HALF], scales[:, jh * HALF : (jh + 1) * HALF])
 
-        ys = [keep.tile([P, S], F32, name="y%d" % t) for t in range(PACK)]
+        ys = {}
 
-        def detect(t, c):
-            bank = zbank.tile([P, CH], F32, name="zb", tag="zb")
+        def y_tile(t, c0, c1, tag):
+            y = keep.tile([P, (c1 - c0) * CH], F32, name="y%d_%d" % (t, c0), tag=tag or "y%d_%d" % (t, c0), align_bytes=64)
+            for c in range(c0, c1):
+                ys[t, c] = y[:, (c - c0) * CH : (c - c0 + 1) * CH]
+            ys[t, c0, c1] = y[:]
+
+        def detect(t, c, side):
+            bank = hbank.tile([P, CH], F32, name="zb", tag=side)
             for jh in range(2):
                 for a in range(2):
                     codes, scales = hq[c, a, jh]
@@ -236,23 +257,30 @@ def tile_list_hologram_detector_page_kernel(
                         start=(a == 0),
                         stop=(a == 1),
                     )
-            nc.scalar.activation(ys[t][:, c * CH : (c + 1) * CH], bank[:], ACT.Tanh)
+            nc.scalar.activation(ys[t, c], bank[:], ACT.Tanh)
+
+        wg_first, wg_rest = {}, {}
+
+        def weights_first(t):
+            wg = keep.tile([P, CH], F32, name="wg_first%d" % t, tag="wg_first%d" % t)
+            nc.scalar.activation(wg[:], wgo_first[:, t, :], ACT.Copy, scale=gain_sb[:, t : t + 1])
+            wg_first[t] = wg
+
+        def weights_rest(t, tag):
+            wg = keep.tile([P, S - CH], F32, name="wg_rest%d" % t, tag=tag, align_bytes=64)
+            if t < 2:
+                nc.vector.tensor_scalar(wg[:], wgo_rest[t // 2][:, t % 2, :], gain_sb[:, t : t + 1], None, ALU.mult)
+            else:
+                nc.scalar.activation(wg[:], wgo_rest[t // 2][:, t % 2, :], ACT.Copy, scale=gain_sb[:, t : t + 1])
+            wg_rest[t] = wg
 
         def scatter(t, c0, c1):
-            j0, j1 = c0 * CH, c1 * CH
-            wg = ring.tile([P, j1 - j0], F32, name="wg", tag="wg")
-            for p0, width, part in wgo_parts:
-                lo, hi = max(j0, p0), min(j1, p0 + width)
-                if lo < hi:
-                    nc.vector.tensor_scalar(
-                        wg[:, lo - j0 : hi - j0], part[:, t, lo - p0 : hi - p0], gain_sb[:, t : t + 1], None, ALU.mult
-                    )
-            nc.vector.tensor_tensor(
-                pages[t][:].indirect(idx2[:, j0 // 16 : j1 // 16]), ys[t][:, j0:j1], wg[:], ALU.mult
-            )
+            wg = wg_first[t][:] if c0 == 0 else wg_rest[t][:, (c0 - 1) * CH : (c1 - 1) * CH]
+            nc.vector.tensor_tensor(pages[t][:].indirect(idx2[:, c0 * CH // 16 : c1 * CH // 16]), ys[t, c0, c1], wg, ALU.mult)
 
-        def detect_scatter(t, c):
-            detect(t, c)
+        def detect_scatter(t, c, side, tag=None):
+            y_tile(t, c, c + 1, tag if HOLD else None)
+            detect(t, c, side)
             scatter(t, c, c + 1)
 
         out_rows = out_0.rearrange("(p t) m -> p t m", t=PACK)
@@ -266,33 +294,45 @@ def tile_list_hologram_detector_page_kernel(
         def finish_page(t):
             nc.sync.dma_start(out_rows[:, t, :], pages[t][:])
             for m0, width, pair in pairs:
-                nc.scalar.copy(pair[:, t // 2, :, t % 2], pages[t][:, m0 : m0 + width])
+                if TAIL_STYLE == "pairs":
+                    nc.scalar.copy(pair[:, t // 2, :, t % 2], pages[t][:, m0 : m0 + width])
+                else:
+                    pl = pair[:].rearrange("p u m e -> p (u m e)").rearrange("p (t m) -> p t m", t=PACK)
+                    nc.scalar.copy(pl[:, t, :], pages[t][:, m0 : m0 + width])
 
         field_first(0)
         field_first(1)
+        gw1.append(keep.tile([P, S // 2], U32, name="gw1_1", tag="hg0_1_1", align_bytes=64))
+        nc.vector.tensor_copy(gw1[1][:], tw[1][:].indirect(idx[:, 32:64]))
         field(1, 0)
-        detect_scatter(0, 0)
-        detect_scatter(1, 0)
+        for t in range(PACK):
+            weights_first(t)
+        y_tile(2, 1, 4, None)
+        y_tile(3, 1, 4, None)
+        detect_scatter(0, 0, "zb0")
+        detect_scatter(1, 0, "zb1")
         field(1, 1)
-        detect_scatter(2, 0)
-        detect_scatter(3, 0)
-        field(2, 0)
-        detect_scatter(0, 1)
-        detect_scatter(1, 1)
-        field(2, 1)
-        detect_scatter(2, 1)
+        detect_scatter(2, 0, "zb0", "hplanes1_1")
+        detect_scatter(3, 0, "zb0")
+        field(2, 0, 0)
+        detect_scatter(0, 1, "zb1")
+        field(2, 1, 1)
+        detect_scatter(1, 1, "zb0")
         field(3, 0)
-        detect_scatter(0, 2)
-        detect_scatter(1, 2)
+        detect_scatter(0, 2, "zb1")
         field(3, 1)
-        detect(2, 2)
-        detect(3, 1)
-        detect(3, 2)
-        detect_scatter(0, 3)
-        detect_scatter(1, 3)
-        detect(2, 3)
-        scatter(2, 2, 4)
-        detect(3, 3)
+        detect_scatter(1, 2, "zb0", "hplanes3_1")
+        detect(2, 1, "zb1")
+        detect(2, 2, "zb1")
+        detect(3, 1, "zb1")
+        detect(3, 2, "zb1")
+        detect_scatter(0, 3, "hb2_0")
+        detect_scatter(1, 3, "hb2_1")
+        detect(2, 3, "hb0_0")
+        detect(3, 3, "hb0_1")
+        weights_rest(2, "hg1_1")
+        scatter(2, 1, 4)
+        weights_rest(3, "hplanes3_1")
         scatter(3, 1, 4)
         for t in range(PACK):
             finish_page(t)
@@ -301,10 +341,18 @@ def tile_list_hologram_detector_page_kernel(
         words_out = out_1[0].rearrange("p m t -> p (m t)")
         for n, (m0, width, pair) in enumerate(pairs):
             yg = keep.tile([P, width, PACK], BF16, name="yg%d" % n, align_bytes=64)
-            nc.vector.tensor_copy(
-                yg[:].rearrange("p m t -> p (m t)").bitcast(I32).rearrange("p (m u) -> p m u", u=2),
-                pair[:].rearrange("p u m e -> p u (m e)").bitcast(I32).rearrange("p u m -> p m u"),
-            )
+            if TAIL_STYLE == "pairs":
+                nc.vector.tensor_copy(
+                    yg[:].rearrange("p m t -> p (m t)").bitcast(I32).rearrange("p (m u) -> p m u", u=2),
+                    pair[:].rearrange("p u m e -> p u (m e)").bitcast(I32).rearrange("p u m -> p m u"),
+                )
+            else:
+                pl = pair[:].rearrange("p u m e -> p (u m e)").rearrange("p (t c i) -> p c t i", t=PACK, i=4)
+                dst = yg[:].rearrange("p (c i) t -> p c t i", i=4)
+                if n in TAIL_SCALAR:
+                    nc.scalar.copy(dst, pl)
+                else:
+                    nc.vector.tensor_copy(dst, pl)
             ywords = keep.tile([P, width], U32, name="ywords%d" % n, align_bytes=64)
             nc.vector.quantize_mx(
                 out=ywords[:].bitcast(FP8X4), scales=yscales[:, m0 : m0 + width], in_=yg[:].rearrange("p m t -> p (m t)")

@@ -24,9 +24,10 @@ NCH = S // CH
 HALF = 128
 TAIL = [256, 512, 512, 512, 256]
 TAIL_STYLE = "pairs"
-TAIL_SCALAR = ()
+TAIL_SCALAR = (3,)
 WD16 = True
 HOLD = True
+WGO_PARTS = ((0, 0, 1), (1, 0, 1), (0, 1, 2), (0, 2, 4), (1, 1, 4))
 
 
 def tile_list_hologram_detector_page_kernel(
@@ -57,7 +58,9 @@ def tile_list_hologram_detector_page_kernel(
 
         def load_table(a):
             t_a = keep.tile([P, T], U32, name="tw%d" % a, align_bytes=64)
-            nc.sync.dma_start(t_a[:].bitcast(I32), tab_words[a].rearrange("p n t -> p (n t)").bitcast(I32))
+            words = tab_words[a].rearrange("p n t -> p (n t)").bitcast(I32)
+            for h in range(2):
+                nc.sync.dma_start(t_a[:, h * 1024 : (h + 1) * 1024].bitcast(I32), words[:, h * 1024 : (h + 1) * 1024])
             return t_a
 
         ref_sb = keep.tile([P, 2, 2 * PACK], F32, name="ref_sb")
@@ -69,33 +72,32 @@ def tile_list_hologram_detector_page_kernel(
         nc.sync.dma_start(gain_sb[:], gain.rearrange("(p t) -> p t", t=PACK))
         for a in range(2):
             nc.sync.dma_start(wd_raw[:, a, :].bitcast(I32), wd_words[a].bitcast(I32))
-        pc_a0 = load_cols(pc, 0, CH, "pc_a0", "pc_a0")
-        pc_a1 = load_cols(pc, CH, CH, "pc_a1", "pc_a1")
+        pc_a0 = load_cols(pc, 0, CH, "pc_a0", "pc_a0_page2")
+        pc_a1 = load_cols(pc, CH, CH, "pc_a1", "pc_a1_page3")
         for q in range(4):
             nc.sync.dma_start(tsc[32 * q : 32 * q + 8, :].bitcast(I32), tab_scales[:, 4 * q : 4 * q + 4, :].bitcast(I32))
         tw = [load_table(0)]
+        ps_a0 = load_cols(ps, 0, CH, "ps_a0", "ps_a0")
+        ps_a1 = load_cols(ps, CH, CH, "ps_a1", "ps_a1")
+        tw.append(load_table(1))
+        pc_b0 = load_cols(pc, 2 * CH, CH, "pc_b0", "pc_b0")
+        pc_b1 = load_cols(pc, 3 * CH, CH, "pc_b1", "pc_b1")
+        ps_b0 = load_cols(ps, 2 * CH, CH, "ps_b0", "hplanes1_0")
+        ps_b1 = load_cols(ps, 3 * CH, CH, "ps_b1", "ps_b1")
         for q in range(4):
             nc.sync.dma_start(
                 wsc_raw[32 * q : 32 * q + 4, :, :].bitcast(I32),
                 wd_scales[:, 4 * q : 4 * q + 4, :].rearrange("a r n -> r a n").bitcast(I32),
             )
-        ps_a = load_cols(ps, 0, BLK, "ps_a", "ps_a")
-        tw.append(load_table(1))
-        pc_b0 = load_cols(pc, 2 * CH, CH, "pc_b0", "pc_b0")
-        pc_b1 = load_cols(pc, 3 * CH, CH, "pc_b1", "pc_b1_page2")
-        ps_b0 = load_cols(ps, 2 * CH, CH, "ps_b0", "hplanes1_0")
-        ps_b1 = load_cols(ps, 3 * CH, CH, "ps_b1", "ps_b1_page3")
 
         wgo_rows = wgo.rearrange("(q t) j -> q t j", t=PACK)
-        wgo_first = keep.tile([P, PACK, CH], F32, name="wgo_first")
-        for q in (0, 2, 1, 3):
-            nc.sync.dma_start(wgo_first[32 * q : 32 * q + 32, :, :], wgo_rows[:, :, 0:CH])
-        wgo_rest = []
-        for u in range(2):
-            part = keep.tile([P, 2, S - CH], F32, name="wgo_rest%d" % u)
+        wgo_sb = {}
+        for u, c0, c1 in WGO_PARTS:
+            part = keep.tile([P, 2, (c1 - c0) * CH], F32, name="wgo%d_%d" % (u, c0), tag="wgo%d_%d" % (u, c0))
             for q in (0, 2, 1, 3):
-                nc.sync.dma_start(part[32 * q : 32 * q + 32, :, :], wgo_rows[:, 2 * u : 2 * u + 2, CH:S])
-            wgo_rest.append(part)
+                nc.sync.dma_start(part[32 * q : 32 * q + 32, :, :], wgo_rows[:, 2 * u : 2 * u + 2, c0 * CH : c1 * CH])
+            for e in range(2):
+                wgo_sb[2 * u + e, c0] = (part[:, e, :], c1)
 
         pages = []
         for t in range(2):
@@ -114,8 +116,8 @@ def tile_list_hologram_detector_page_kernel(
             return gw1[j0 // 512][:, j0 % 512 : j0 % 512 + width]
 
         def deal(engine, grouped, raw, c0, m0, negate):
-            dst = grouped[:, :, m0 : m0 + 64, :].rearrange("p t m i -> p m i t")
-            src = raw[:, :, c0 : c0 + 256].rearrange("p i (m t) -> p m i t", t=PACK)
+            dst = grouped[:, :, m0 : m0 + 64, :].rearrange("p t m i -> p m t i")
+            src = raw[:, :, c0 : c0 + 256].rearrange("p i (m t) -> p m t i", t=PACK)
             if engine == "scalar":
                 nc.scalar.activation(dst, src, ACT.Copy, scale=-1.0 if negate else 1.0)
             elif negate:
@@ -123,20 +125,19 @@ def tile_list_hologram_detector_page_kernel(
             else:
                 nc.vector.tensor_copy(dst, src)
 
-        def quantise(src, width, name, pool, tag):
-            codes = pool.tile([P, width], U32, name=name + "_codes", tag=tag + "_codes", align_bytes=64)
+        def quantise(src, width, name, pool, tag, codes_tag=None):
+            codes = pool.tile([P, width], U32, name=name + "_codes", tag=codes_tag or tag + "_codes", align_bytes=64)
             scales = pool.tile([P, width], U8, name=name + "_scales", tag=tag + "_scales", align_bytes=64)
             nc.vector.quantize_mx(out=codes[:].bitcast(FP8X4), scales=scales[:], in_=src)
             return codes, scales
 
         def new_grouped(name):
-            return keep.tile([P, PACK, P, PACK], BF16, name=name, align_bytes=64)
+            return keep.tile([P, PACK, P, PACK], BF16, name=name, tag=name, align_bytes=64)
 
         def flat(grouped):
             return grouped[:].rearrange("p t m i -> p (t m i)")
 
         wd = keep.tile([P, 2, PACK, P, 2], U8, name="wd", align_bytes=64)
-        wsc = keep.tile([P, 2, PACK, P], U8, name="wsc", align_bytes=64)
         for a in range(2):
             if WD16:
                 nc.vector.tensor_copy(
@@ -152,29 +153,29 @@ def tile_list_hologram_detector_page_kernel(
         g = new_grouped("g_pc_a")
         deal("scalar", g, pc_a0, 0, 0, False)
         deal("scalar", g, pc_a1, 0, 64, False)
+        for t, tag in ((2, "pc_a0_page2"), (3, "pc_a1_page3")):
+            page = keep.tile([P, T2], F32, name="page%d" % t, tag=tag, align_bytes=64)
+            for h in range(8):
+                nc.gpsimd.memset(page[:, h * 256 : (h + 1) * 256], 0.0)
+            pages.append(page)
         nc.vector.tensor_copy(gs[:], tsc[:].indirect(idx[:]))
         nc.vector.tensor_copy(gw0[:], tw[0][:].indirect(idx[:]))
         prop[0, 0] = quantise(flat(g), BLK, "pc_a", keep, "pc_a")
         g = new_grouped("g_ps_a")
-        deal("scalar", g, ps_a, 0, 0, True)
-        deal("scalar", g, ps_a, CH, 64, True)
+        deal("scalar", g, ps_a0, 0, 0, True)
+        deal("scalar", g, ps_a1, 0, 64, True)
         prop[1, 0] = quantise(flat(g), BLK, "ps_a", keep, "ps_a")
         nc.vector.tensor_copy(gw1[0][:], tw[1][:].indirect(idx[:, 0:32]))
         g = new_grouped("g_pc_b")
         deal("scalar", g, pc_b0, 0, 0, False)
         deal("scalar", g, pc_b1, 0, 64, False)
-        prop[0, 1] = quantise(flat(g), BLK, "pc_b", keep, "pc_b")
+        prop[0, 1] = quantise(flat(g), BLK, "pc_b", keep, "pc_b", "g_ps_a")
         g = new_grouped("g_ps_b")
         deal("scalar", g, ps_b0, 0, 0, True)
         deal("vector", g, ps_b1, 0, 64, True)
         prop[1, 1] = quantise(flat(g), BLK, "ps_b", keep, "ps_b")
+        wsc = keep.tile([P, 2, PACK, P], U8, name="wsc", tag="g_ps_b", align_bytes=64)
         nc.vector.tensor_copy(wsc[:].rearrange("p a t m -> p a m t"), wsc_raw[:].rearrange("p a (m t) -> p a m t", t=PACK))
-
-        for t, tag in ((2, "pc_b1_page2"), (3, "ps_b1_page3")):
-            page = keep.tile([P, T2], F32, name="page%d" % t, tag=tag, align_bytes=64)
-            for h in range(8):
-                nc.gpsimd.memset(page[:, h * 256 : (h + 1) * 256], 0.0)
-            pages.append(page)
 
         def field_pass(out, a, b, t, j0, width, start, stop):
             codes, scales = prop[a, b]
@@ -214,7 +215,7 @@ def tile_list_hologram_detector_page_kernel(
                 codes, scales = quantise(hg[jh][:].rearrange("p j t -> p (j t)"), HALF, name, keep, name)
                 hq[0, b, jh] = (codes[:], scales[:])
 
-        def field(c, b, t_rest=None):
+        def field(c, b, part=None):
             planes = keep.tile([P, PACK, CH], BF16, name="hplanes", tag="hplanes%d_%d" % (c, b), align_bytes=64)
             for u in range(2):
                 bank = hbank.tile([P, 2, CH], F32, name="hb", tag="hb%d_%d" % ((2 * c + b) % 3, u))
@@ -228,8 +229,8 @@ def tile_list_hologram_detector_page_kernel(
             nc.scalar.copy(
                 hg[:].rearrange("p (c i) t -> p c t i", i=4), planes[:].rearrange("p t (c i) -> p c t i", i=4)
             )
-            if t_rest is not None:
-                weights_rest(t_rest, "hplanes%d_%d" % (c, b))
+            if part is not None:
+                weights("vector", part[0], part[1], "hplanes%d_%d" % (c, b))
             name = "h%d_%d" % (c, b)
             codes, scales = quantise(hg[:].rearrange("p j t -> p (j t)"), CH, name, keep, name)
             for jh in range(2):
@@ -259,24 +260,27 @@ def tile_list_hologram_detector_page_kernel(
                     )
             nc.scalar.activation(ys[t, c], bank[:], ACT.Tanh)
 
-        wg_first, wg_rest = {}, {}
+        wgs = {}
 
-        def weights_first(t):
-            wg = keep.tile([P, CH], F32, name="wg_first%d" % t, tag="wg_first%d" % t)
-            nc.scalar.activation(wg[:], wgo_first[:, t, :], ACT.Copy, scale=gain_sb[:, t : t + 1])
-            wg_first[t] = wg
-
-        def weights_rest(t, tag):
-            wg = keep.tile([P, S - CH], F32, name="wg_rest%d" % t, tag=tag, align_bytes=64)
-            if t < 2:
-                nc.vector.tensor_scalar(wg[:], wgo_rest[t // 2][:, t % 2, :], gain_sb[:, t : t + 1], None, ALU.mult)
+        def weights(engine, t, c0, tag=None):
+            src, c1 = wgo_sb[t, c0]
+            name = "wg%d_%d" % (t, c0)
+            wg = keep.tile([P, (c1 - c0) * CH], F32, name=name, tag=tag or name, align_bytes=64)
+            if engine == "vector":
+                nc.vector.tensor_scalar(wg[:], src, gain_sb[:, t : t + 1], None, ALU.mult)
             else:
-                nc.scalar.activation(wg[:], wgo_rest[t // 2][:, t % 2, :], ACT.Copy, scale=gain_sb[:, t : t + 1])
-            wg_rest[t] = wg
+                nc.scalar.activation(wg[:], src, ACT.Copy, scale=gain_sb[:, t : t + 1])
+            for c in range(c0, c1):
+                wgs[t, c] = (wg, (c - c0) * CH)
 
         def scatter(t, c0, c1):
-            wg = wg_first[t][:] if c0 == 0 else wg_rest[t][:, (c0 - 1) * CH : (c1 - 1) * CH]
-            nc.vector.tensor_tensor(pages[t][:].indirect(idx2[:, c0 * CH // 16 : c1 * CH // 16]), ys[t, c0, c1], wg, ALU.mult)
+            wg, j0 = wgs[t, c0]
+            nc.vector.tensor_tensor(
+                pages[t][:].indirect(idx2[:, c0 * CH // 16 : c1 * CH // 16]),
+                ys[t, c0, c1],
+                wg[:, j0 : j0 + (c1 - c0) * CH],
+                ALU.mult,
+            )
 
         def detect_scatter(t, c, side, tag=None):
             y_tile(t, c, c + 1, tag if HOLD else None)
@@ -284,12 +288,6 @@ def tile_list_hologram_detector_page_kernel(
             scatter(t, c, c + 1)
 
         out_rows = out_0.rearrange("(p t) m -> p t m", t=PACK)
-        pairs = []
-        m0 = 0
-        for n, width in enumerate(TAIL):
-            pair = keep.tile([P, 2, width, 2], BF16, name="pair%d" % n)
-            pairs.append((m0, width, pair))
-            m0 = m0 + width
 
         def finish_page(t):
             nc.sync.dma_start(out_rows[:, t, :], pages[t][:])
@@ -306,34 +304,42 @@ def tile_list_hologram_detector_page_kernel(
         nc.vector.tensor_copy(gw1[1][:], tw[1][:].indirect(idx[:, 32:64]))
         field(1, 0)
         for t in range(PACK):
-            weights_first(t)
+            weights("scalar", t, 0)
         y_tile(2, 1, 4, None)
         y_tile(3, 1, 4, None)
         detect_scatter(0, 0, "zb0")
         detect_scatter(1, 0, "zb1")
         field(1, 1)
         detect_scatter(2, 0, "zb0", "hplanes1_1")
-        detect_scatter(3, 0, "zb0")
-        field(2, 0, 0)
-        detect_scatter(0, 1, "zb1")
-        field(2, 1, 1)
-        detect_scatter(1, 1, "zb0")
-        field(3, 0)
-        detect_scatter(0, 2, "zb1")
+        detect_scatter(3, 0, "zb1")
+        field(2, 0, (0, 1))
+        detect_scatter(0, 1, "zb0")
+        field(2, 1, (1, 1))
+        detect_scatter(1, 1, "zb1")
+        field(3, 0, (0, 2))
+        detect_scatter(0, 2, "zb0")
+        weights("vector", 1, 2, "hg1_0")
         field(3, 1)
-        detect_scatter(1, 2, "zb0", "hplanes3_1")
-        detect(2, 1, "zb1")
-        detect(2, 2, "zb1")
-        detect(3, 1, "zb1")
-        detect(3, 2, "zb1")
-        detect_scatter(0, 3, "hb2_0")
-        detect_scatter(1, 3, "hb2_1")
-        detect(2, 3, "hb0_0")
-        detect(3, 3, "hb0_1")
-        weights_rest(2, "hg1_1")
+        detect_scatter(1, 2, "zb1", "hplanes3_1")
+        detect_scatter(0, 3, "zb0")
+        detect_scatter(1, 3, "hb1_0")
+        detect(2, 1, "hb2_0")
+        detect(3, 1, "hb2_1")
+        detect(2, 2, "hb0_0")
+        detect(3, 2, "hb0_1")
+        detect(2, 3, "hb1_1")
+        detect(3, 3, "zb1")
+        weights("scalar", 2, 1, "hg1_1")
         scatter(2, 1, 4)
-        weights_rest(3, "hplanes3_1")
+        weights("scalar", 3, 1, "hplanes3_1")
         scatter(3, 1, 4)
+        pairs = []
+        pair_row = keep.tile([P, PACK * T2], BF16, name="pair_row", tag="wgo1_1")
+        m0 = 0
+        for n, width in enumerate(TAIL):
+            pair = pair_row[:, PACK * m0 : PACK * (m0 + width)].rearrange("p (u m e) -> p u m e", u=2, e=2)
+            pairs.append((m0, width, pair))
+            m0 = m0 + width
         for t in range(PACK):
             finish_page(t)
 
@@ -341,7 +347,12 @@ def tile_list_hologram_detector_page_kernel(
         words_out = out_1[0].rearrange("p m t -> p (m t)")
         for n, (m0, width, pair) in enumerate(pairs):
             yg = keep.tile([P, width, PACK], BF16, name="yg%d" % n, align_bytes=64)
-            if TAIL_STYLE == "pairs":
+            if TAIL_STYLE == "pairs" and n in TAIL_SCALAR:
+                nc.scalar.copy(
+                    yg[:].rearrange("p m t -> p (m t)").bitcast(F32).rearrange("p (m u) -> p m u", u=2),
+                    pair[:].rearrange("p u m e -> p u (m e)").bitcast(F32).rearrange("p u m -> p m u"),
+                )
+            elif TAIL_STYLE == "pairs":
                 nc.vector.tensor_copy(
                     yg[:].rearrange("p m t -> p (m t)").bitcast(I32).rearrange("p (m u) -> p m u", u=2),
                     pair[:].rearrange("p u m e -> p u (m e)").bitcast(I32).rearrange("p u m -> p m u"),

@@ -2,7 +2,7 @@ from contextlib import ExitStack
 
 import concourse.mybir as mybir
 
-K, C, R, N, T, S, T2 = 1024, 512, 1024, 512, 2048, 1024, 2048
+K, R, N, T, S, T2 = 1024, 1024, 512, 2048, 1024, 2048
 FLOPS = 2 * K * R * S + 2 * R * N * S
 
 F32 = mybir.dt.float32
@@ -18,16 +18,15 @@ ALU = mybir.AluOpType
 
 P = 128
 PACK = 4
-BLK = 512
+QUADS = 4
+BLK = P * PACK
 CH = 256
-NCH = S // CH
 HALF = 128
-TAIL = [256, 512, 512, 512, 256]
-TAIL_STYLE = "pairs"
-TAIL_SCALAR = (3,)
-WD16 = True
-HOLD = True
+PER_COL = 16
 WGO_PARTS = ((0, 0, 1), (1, 0, 1), (0, 1, 2), (0, 2, 4), (1, 1, 4))
+SHORT, LONG = 256, 512
+TAIL = (SHORT, SHORT, LONG, LONG, SHORT, SHORT)
+TAIL_ON_VECTOR = 4
 
 
 def tile_list_hologram_detector_page_kernel(
@@ -36,98 +35,98 @@ def tile_list_hologram_detector_page_kernel(
     nc = tc.nc
     with ExitStack() as ctx:
         keep = ctx.enter_context(tc.tile_pool(name="keep", bufs=1))
-        hbank = ctx.enter_context(tc.psum_pool(name="hbank", bufs=1))
+        psum = ctx.enter_context(tc.psum_pool(name="psum", bufs=1))
 
-        idx = keep.tile([P, S // 16], U16, name="idx")
-        idx2 = keep.tile([P, S // 16], U16, name="idx2")
+        idx = keep.tile([P, S // PER_COL], U16, name="idx")
+        idx2 = keep.tile([P, S // PER_COL], U16, name="idx2")
         nc.sync.dma_start(idx[:], offs)
 
-        tsc = keep.tile([P, T], U8, name="tsc", tag="pc_a_codes", align_bytes=64)
-        wsc_raw = keep.tile([P, 2, N], U8, name="wsc_raw", align_bytes=64)
-        nc.gpsimd.memset(tsc[:].bitcast(I32), 0)
-        nc.gpsimd.memset(wsc_raw[:].bitcast(I32), 0)
+        tab_sc = keep.tile([P, T], U8, name="tab_sc", tag="pc0_codes", align_bytes=64)
+        wd_sc_raw = keep.tile([P, 2, N], U8, name="wd_sc_raw", align_bytes=64)
+        nc.gpsimd.memset(tab_sc[:].bitcast(I32), 0)
+        nc.gpsimd.memset(wd_sc_raw[:].bitcast(I32), 0)
 
-        warm = keep.tile([P, 8], F32, name="warm")
-        nc.vector.memset(warm[:, 0:1], 0.0)
-        nc.scalar.activation(warm[:, 1:2], warm[:, 0:1], ACT.Tanh)
-
-        def load_cols(src, c0, width, name, tag):
-            raw = keep.tile([P, PACK, width], F32, name=name, tag=tag, align_bytes=64)
-            nc.sync.dma_start(raw[:], src.rearrange("(p i) r -> p i r", i=PACK)[:, :, c0 : c0 + width])
+        def load_cols(src, part, name, tag=None):
+            raw = keep.tile([P, PACK, CH], F32, name=name, tag=tag or name, align_bytes=64)
+            nc.sync.dma_start(raw[:], src.rearrange("(p i) r -> p i r", i=PACK)[:, :, part * CH : (part + 1) * CH])
             return raw
 
-        def load_table(a):
-            t_a = keep.tile([P, T], U32, name="tw%d" % a, align_bytes=64)
+        def load_table(a, pieces):
+            tile = keep.tile([P, T], U32, name="tab%d" % a, align_bytes=64)
             words = tab_words[a].rearrange("p n t -> p (n t)").bitcast(I32)
-            for h in range(2):
-                nc.sync.dma_start(t_a[:, h * 1024 : (h + 1) * 1024].bitcast(I32), words[:, h * 1024 : (h + 1) * 1024])
-            return t_a
+            width = T // pieces
+            for h in range(pieces):
+                cols = slice(h * width, (h + 1) * width)
+                nc.sync.dma_start(tile[:, cols].bitcast(I32), words[:, cols])
+            return tile
 
-        ref_sb = keep.tile([P, 2, 2 * PACK], F32, name="ref_sb")
+        ref_sb = keep.tile([P, 2, PACK], F32, name="ref_sb")
         gain_sb = keep.tile([P, PACK], F32, name="gain_sb")
         wd_raw = keep.tile([P, 2, 2 * N], U8, name="wd_raw", align_bytes=64)
         nc.sync.dma_start(idx2[:], offs2)
-        for b in range(2):
-            nc.sync.dma_start(ref_sb[:, b, 0:PACK], ref[b * BLK : (b + 1) * BLK].rearrange("(p t) -> p t", t=PACK))
-        nc.sync.dma_start(gain_sb[:], gain.rearrange("(p t) -> p t", t=PACK))
+        tab = [load_table(0, 2)]
         for a in range(2):
             nc.sync.dma_start(wd_raw[:, a, :].bitcast(I32), wd_words[a].bitcast(I32))
-        pc_a0 = load_cols(pc, 0, CH, "pc_a0", "pc_a0_page2")
-        pc_a1 = load_cols(pc, CH, CH, "pc_a1", "pc_a1_page3")
-        for q in range(4):
-            nc.sync.dma_start(tsc[32 * q : 32 * q + 8, :].bitcast(I32), tab_scales[:, 4 * q : 4 * q + 4, :].bitcast(I32))
-        tw = [load_table(0)]
-        ps_a0 = load_cols(ps, 0, CH, "ps_a0", "ps_a0")
-        ps_a1 = load_cols(ps, CH, CH, "ps_a1", "ps_a1")
-        tw.append(load_table(1))
-        pc_b0 = load_cols(pc, 2 * CH, CH, "pc_b0", "pc_b0")
-        pc_b1 = load_cols(pc, 3 * CH, CH, "pc_b1", "pc_b1")
-        ps_b0 = load_cols(ps, 2 * CH, CH, "ps_b0", "hplanes1_0")
-        ps_b1 = load_cols(ps, 3 * CH, CH, "ps_b1", "ps_b1")
-        for q in range(4):
+        nc.sync.dma_start(ref_sb[:], ref.rearrange("(b p t) -> p b t", b=2, t=PACK))
+        pc_raw = [load_cols(pc, 0, "pc_raw0", "page2")]
+        for q in range(QUADS):
             nc.sync.dma_start(
-                wsc_raw[32 * q : 32 * q + 4, :, :].bitcast(I32),
+                tab_sc[32 * q : 32 * q + 8, :].bitcast(I32), tab_scales[:, 4 * q : 4 * q + 4, :].bitcast(I32)
+            )
+        pc_raw.append(load_cols(pc, 1, "pc_raw1", "page3"))
+        ps_raw = [load_cols(ps, part, "ps_raw%d" % part) for part in range(2)]
+        tab.append(load_table(1, 1))
+        pc_raw.extend(load_cols(pc, part, "pc_raw%d" % part) for part in range(2, 4))
+        ps_raw.append(load_cols(ps, 2, "ps_raw2", "planes1_0"))
+        ps_raw.append(load_cols(ps, 3, "ps_raw3"))
+        for q in range(QUADS):
+            nc.sync.dma_start(
+                wd_sc_raw[32 * q : 32 * q + 4, :, :].bitcast(I32),
                 wd_scales[:, 4 * q : 4 * q + 4, :].rearrange("a r n -> r a n").bitcast(I32),
             )
+        nc.sync.dma_start(gain_sb[:], gain.rearrange("(p t) -> p t", t=PACK))
 
         wgo_rows = wgo.rearrange("(q t) j -> q t j", t=PACK)
         wgo_sb = {}
         for u, c0, c1 in WGO_PARTS:
-            part = keep.tile([P, 2, (c1 - c0) * CH], F32, name="wgo%d_%d" % (u, c0), tag="wgo%d_%d" % (u, c0))
+            name = "wgo%d_%d" % (u, c0)
+            part_tile = keep.tile([P, 2, (c1 - c0) * CH], F32, name=name, tag=name)
             for q in (0, 2, 1, 3):
-                nc.sync.dma_start(part[32 * q : 32 * q + 32, :, :], wgo_rows[:, 2 * u : 2 * u + 2, c0 * CH : c1 * CH])
+                nc.sync.dma_start(
+                    part_tile[32 * q : 32 * q + 32, :, :], wgo_rows[:, 2 * u : 2 * u + 2, c0 * CH : c1 * CH]
+                )
             for e in range(2):
-                wgo_sb[2 * u + e, c0] = (part[:, e, :], c1)
+                wgo_sb[2 * u + e, c0] = (part_tile[:, e, :], c1)
 
         pages = []
         for t in range(2):
             page = keep.tile([P, T2], F32, name="page%d" % t)
             for h in range(2):
-                nc.vector.memset(page[:, h * 1024 : (h + 1) * 1024], 0.0)
+                nc.vector.memset(page[:, h * T2 // 2 : (h + 1) * T2 // 2], 0.0)
             pages.append(page)
 
-        gs = keep.tile([P, S], U8, name="gs", align_bytes=64)
-        gw0 = keep.tile([P, S], U32, name="gw0", align_bytes=64)
-        gw1 = [keep.tile([P, S // 2], U32, name="gw1_0", align_bytes=64)]
+        got_sc = keep.tile([P, S], U8, name="got_sc", align_bytes=64)
+        got0 = keep.tile([P, S], U32, name="got0", align_bytes=64)
+        got1 = [keep.tile([P, S // 2], U32, name="got1_0", align_bytes=64)]
 
         def gathered(a, j0, width):
             if a == 0:
-                return gw0[:, j0 : j0 + width]
-            return gw1[j0 // 512][:, j0 % 512 : j0 % 512 + width]
+                return got0[:, j0 : j0 + width]
+            half, j = divmod(j0, S // 2)
+            return got1[half][:, j : j + width]
 
-        def deal(engine, grouped, raw, c0, m0, negate):
-            dst = grouped[:, :, m0 : m0 + 64, :].rearrange("p t m i -> p m t i")
-            src = raw[:, :, c0 : c0 + 256].rearrange("p i (m t) -> p m t i", t=PACK)
-            if engine == "scalar":
-                nc.scalar.activation(dst, src, ACT.Copy, scale=-1.0 if negate else 1.0)
-            elif negate:
-                nc.vector.tensor_scalar(dst, src, -1.0, None, ALU.mult)
-            else:
-                nc.vector.tensor_copy(dst, src)
+        def deal_views(grouped, raw, half):
+            m = CH // PACK
+            dst = grouped[:, :, half * m : (half + 1) * m, :].rearrange("p t m i -> p m t i")
+            return dst, raw[:].rearrange("p i (m t) -> p m t i", t=PACK)
 
-        def quantise(src, width, name, pool, tag, codes_tag=None):
-            codes = pool.tile([P, width], U32, name=name + "_codes", tag=codes_tag or tag + "_codes", align_bytes=64)
-            scales = pool.tile([P, width], U8, name=name + "_scales", tag=tag + "_scales", align_bytes=64)
+        def deal_scalar(grouped, raw, half, sign):
+            dst, src = deal_views(grouped, raw, half)
+            nc.scalar.activation(dst, src, ACT.Copy, scale=sign)
+
+        def quantise(src, width, name, codes_tag=None):
+            codes = keep.tile([P, width], U32, name=name + "_codes", tag=codes_tag or name + "_codes", align_bytes=64)
+            scales = keep.tile([P, width], U8, name=name + "_scales", align_bytes=64)
             nc.vector.quantize_mx(out=codes[:].bitcast(FP8X4), scales=scales[:], in_=src)
             return codes, scales
 
@@ -139,43 +138,42 @@ def tile_list_hologram_detector_page_kernel(
 
         wd = keep.tile([P, 2, PACK, P, 2], U8, name="wd", align_bytes=64)
         for a in range(2):
-            if WD16:
-                nc.vector.tensor_copy(
-                    wd[:, a].rearrange("p t m e -> p (t m e)").bitcast(U16).rearrange("p (t m) -> p m t", t=PACK),
-                    wd_raw[:, a, :].bitcast(U16).rearrange("p (m t) -> p m t", t=PACK),
-                )
-            else:
-                nc.vector.tensor_copy(
-                    wd[:, a].rearrange("p t m e -> p m t e"), wd_raw[:, a, :].rearrange("p (m t e) -> p m t e", t=PACK, e=2)
-                )
+            nc.vector.tensor_copy(
+                wd[:, a].rearrange("p t m e -> p (t m e)").bitcast(U16).rearrange("p (t m) -> p m t", t=PACK),
+                wd_raw[:, a, :].bitcast(U16).rearrange("p (m t) -> p m t", t=PACK),
+            )
 
         prop = {}
-        g = new_grouped("g_pc_a")
-        deal("scalar", g, pc_a0, 0, 0, False)
-        deal("scalar", g, pc_a1, 0, 64, False)
-        for t, tag in ((2, "pc_a0_page2"), (3, "pc_a1_page3")):
-            page = keep.tile([P, T2], F32, name="page%d" % t, tag=tag, align_bytes=64)
-            for h in range(8):
-                nc.gpsimd.memset(page[:, h * 256 : (h + 1) * 256], 0.0)
+        grouped = new_grouped("pc0_bf16")
+        for half in range(2):
+            deal_scalar(grouped, pc_raw[half], half, 1.0)
+        for t in range(2, PACK):
+            page = keep.tile([P, T2], F32, name="page%d" % t, tag="page%d" % t, align_bytes=64)
+            for c0 in range(0, T2, CH):
+                nc.gpsimd.memset(page[:, c0 : c0 + CH], 0.0)
             pages.append(page)
-        nc.vector.tensor_copy(gs[:], tsc[:].indirect(idx[:]))
-        nc.vector.tensor_copy(gw0[:], tw[0][:].indirect(idx[:]))
-        prop[0, 0] = quantise(flat(g), BLK, "pc_a", keep, "pc_a")
-        g = new_grouped("g_ps_a")
-        deal("scalar", g, ps_a0, 0, 0, True)
-        deal("scalar", g, ps_a1, 0, 64, True)
-        prop[1, 0] = quantise(flat(g), BLK, "ps_a", keep, "ps_a")
-        nc.vector.tensor_copy(gw1[0][:], tw[1][:].indirect(idx[:, 0:32]))
-        g = new_grouped("g_pc_b")
-        deal("scalar", g, pc_b0, 0, 0, False)
-        deal("scalar", g, pc_b1, 0, 64, False)
-        prop[0, 1] = quantise(flat(g), BLK, "pc_b", keep, "pc_b", "g_ps_a")
-        g = new_grouped("g_ps_b")
-        deal("scalar", g, ps_b0, 0, 0, True)
-        deal("vector", g, ps_b1, 0, 64, True)
-        prop[1, 1] = quantise(flat(g), BLK, "ps_b", keep, "ps_b")
-        wsc = keep.tile([P, 2, PACK, P], U8, name="wsc", tag="g_ps_b", align_bytes=64)
-        nc.vector.tensor_copy(wsc[:].rearrange("p a t m -> p a m t"), wsc_raw[:].rearrange("p a (m t) -> p a m t", t=PACK))
+        nc.vector.tensor_copy(got0[:], tab[0][:].indirect(idx[:]))
+        nc.vector.tensor_copy(got_sc[:], tab_sc[:].indirect(idx[:]))
+        prop[0, 0] = quantise(flat(grouped), BLK, "pc0")
+        grouped = new_grouped("ps0_bf16")
+        for half in range(2):
+            deal_scalar(grouped, ps_raw[half], half, -1.0)
+        prop[1, 0] = quantise(flat(grouped), BLK, "ps0")
+        half_cols = S // 2 // PER_COL
+        nc.vector.tensor_copy(got1[0][:], tab[1][:].indirect(idx[:, 0:half_cols]))
+        grouped = new_grouped("pc1_bf16")
+        for half in range(2):
+            deal_scalar(grouped, pc_raw[2 + half], half, 1.0)
+        prop[0, 1] = quantise(flat(grouped), BLK, "pc1", "ps0_bf16")
+        grouped = new_grouped("ps1_bf16")
+        deal_scalar(grouped, ps_raw[2], 0, -1.0)
+        dst, src = deal_views(grouped, ps_raw[3], 1)
+        nc.vector.tensor_scalar(dst, src, -1.0, None, ALU.mult)
+        prop[1, 1] = quantise(flat(grouped), BLK, "ps1")
+        wd_sc = keep.tile([P, 2, PACK, P], U8, name="wd_sc", tag="ps1_bf16", align_bytes=64)
+        nc.vector.tensor_copy(
+            wd_sc[:].rearrange("p a t m -> p a m t"), wd_sc_raw[:].rearrange("p a (m t) -> p a m t", t=PACK)
+        )
 
         def field_pass(out, a, b, t, j0, width, start, stop):
             codes, scales = prop[a, b]
@@ -184,133 +182,120 @@ def tile_list_hologram_detector_page_kernel(
                 lhsT=codes[:, t * P : (t + 1) * P].bitcast(FP8X4),
                 lhsT_scale=scales[:, t * P : (t + 1) * P],
                 rhs=gathered(a, j0, width).bitcast(FP8X4),
-                rhs_scale=gs[4 * a : P, j0 : j0 + width],
+                rhs_scale=got_sc[4 * a : P, j0 : j0 + width],
                 start=start,
                 stop=stop,
             )
 
-        hq = {}
+        h_mx = {}
 
         def field_first(b):
-            banks = []
-            for jh in range(2):
-                bank = hbank.tile([P, PACK, HALF], F32, name="hb", tag="hb%d_%d" % (b, jh))
-                banks.append(bank)
+            banks = [psum.tile([P, PACK, HALF], F32, name="h_bank", tag="hb%d_%d" % (b, jh)) for jh in range(2)]
             for a in range(2):
                 for jh in range(2):
                     for t in range(PACK):
-                        field_pass(banks[jh][:, t, :], a, b, t, jh * HALF, HALF, a == 0 and t == 0, a == 1 and t == PACK - 1)
-            hg = []
+                        first, last = a == 0 and t == 0, a == 1 and t == PACK - 1
+                        field_pass(banks[jh][:, t, :], a, b, t, jh * HALF, HALF, first, last)
+            woven = []
             for jh in range(2):
-                hgj = keep.tile([P, HALF, PACK], BF16, name="hg0_%d_%d" % (b, jh), tag="hg0_%d_%d" % (b, jh), align_bytes=64)
+                name = "first%d_%d" % (b, jh)
+                tile = keep.tile([P, HALF, PACK], BF16, name=name, tag=name, align_bytes=64)
                 nc.vector.tensor_tensor(
-                    hgj[:],
+                    tile[:],
                     banks[jh][:].rearrange("p t j -> p j t"),
-                    ref_sb[:, b : b + 1, 0:PACK].to_broadcast([P, HALF, PACK]),
+                    ref_sb[:, b : b + 1, :].to_broadcast([P, HALF, PACK]),
                     ALU.add,
                 )
-                hg.append(hgj)
+                woven.append(tile)
             for jh in range(2):
-                name = "h0_%d_%d" % (b, jh)
-                codes, scales = quantise(hg[jh][:].rearrange("p j t -> p (j t)"), HALF, name, keep, name)
-                hq[0, b, jh] = (codes[:], scales[:])
+                codes, scales = quantise(woven[jh][:].rearrange("p j t -> p (j t)"), HALF, "h0_%d_%d" % (b, jh))
+                h_mx[0, b, jh] = (codes[:], scales[:])
 
-        def field(c, b, part=None):
-            planes = keep.tile([P, PACK, CH], BF16, name="hplanes", tag="hplanes%d_%d" % (c, b), align_bytes=64)
+        def field(c, b, weight_part=None):
+            planes_tag = "planes%d_%d" % (c, b)
+            planes = keep.tile([P, PACK, CH], BF16, name="planes", tag=planes_tag, align_bytes=64)
             for u in range(2):
-                bank = hbank.tile([P, 2, CH], F32, name="hb", tag="hb%d_%d" % ((2 * c + b) % 3, u))
+                bank = psum.tile([P, 2, CH], F32, name="h_bank", tag="hb%d_%d" % ((2 * c + b) % 3, u))
                 for e in range(2):
                     for a in range(2):
                         field_pass(bank[:, e, :], a, b, 2 * u + e, c * CH, CH, a == 0, a == 1)
                 for e in range(2):
                     t = 2 * u + e
                     nc.scalar.activation(planes[:, t, :], bank[:, e, :], ACT.Identity, bias=ref_sb[:, b, t : t + 1])
-            hg = keep.tile([P, CH, PACK], BF16, name="hg", tag="hg%d_%d" % (c % 2, b), align_bytes=64)
+            woven = keep.tile([P, CH, PACK], BF16, name="woven", tag="woven%d_%d" % (c % 2, b), align_bytes=64)
             nc.scalar.copy(
-                hg[:].rearrange("p (c i) t -> p c t i", i=4), planes[:].rearrange("p t (c i) -> p c t i", i=4)
+                woven[:].rearrange("p (c i) t -> p c t i", i=4), planes[:].rearrange("p t (c i) -> p c t i", i=4)
             )
-            if part is not None:
-                weights("vector", part[0], part[1], "hplanes%d_%d" % (c, b))
-            name = "h%d_%d" % (c, b)
-            codes, scales = quantise(hg[:].rearrange("p j t -> p (j t)"), CH, name, keep, name)
+            if weight_part is not None:
+                weights(nc.vector, weight_part[0], weight_part[1], planes_tag)
+            codes, scales = quantise(woven[:].rearrange("p j t -> p (j t)"), CH, "h%d_%d" % (c, b))
             for jh in range(2):
-                hq[c, b, jh] = (codes[:, jh * HALF : (jh + 1) * HALF], scales[:, jh * HALF : (jh + 1) * HALF])
+                cols = slice(jh * HALF, (jh + 1) * HALF)
+                h_mx[c, b, jh] = (codes[:, cols], scales[:, cols])
 
-        ys = {}
+        y_chunk, y_run, wg_sb = {}, {}, {}
 
-        def y_tile(t, c0, c1, tag):
-            y = keep.tile([P, (c1 - c0) * CH], F32, name="y%d_%d" % (t, c0), tag=tag or "y%d_%d" % (t, c0), align_bytes=64)
+        def y_tile(t, c0, c1, tag=None):
+            name = "y%d_%d" % (t, c0)
+            y = keep.tile([P, (c1 - c0) * CH], F32, name=name, tag=tag or name, align_bytes=64)
             for c in range(c0, c1):
-                ys[t, c] = y[:, (c - c0) * CH : (c - c0 + 1) * CH]
-            ys[t, c0, c1] = y[:]
+                y_chunk[t, c] = y[:, (c - c0) * CH : (c - c0 + 1) * CH]
+            y_run[t, c0] = y[:]
 
-        def detect(t, c, side):
-            bank = hbank.tile([P, CH], F32, name="zb", tag=side)
+        def detect(t, c, bank_tag):
+            bank = psum.tile([P, CH], F32, name="z_bank", tag=bank_tag)
             for jh in range(2):
-                for a in range(2):
-                    codes, scales = hq[c, a, jh]
+                for b in range(2):
+                    codes, scales = h_mx[c, b, jh]
                     nc.tensor.matmul_mx(
                         out=bank[:, jh * HALF : (jh + 1) * HALF],
-                        lhsT=wd[:, a, t].rearrange("p m e -> p (m e)").bitcast(FP4X4),
-                        lhsT_scale=wsc[:, a, t, :],
+                        lhsT=wd[:, b, t].rearrange("p m e -> p (m e)").bitcast(FP4X4),
+                        lhsT_scale=wd_sc[:, b, t, :],
                         rhs=codes.bitcast(FP8X4),
                         rhs_scale=scales,
-                        start=(a == 0),
-                        stop=(a == 1),
+                        start=(b == 0),
+                        stop=(b == 1),
                     )
-            nc.scalar.activation(ys[t, c], bank[:], ACT.Tanh)
-
-        wgs = {}
+            nc.scalar.activation(y_chunk[t, c], bank[:], ACT.Tanh)
 
         def weights(engine, t, c0, tag=None):
             src, c1 = wgo_sb[t, c0]
             name = "wg%d_%d" % (t, c0)
             wg = keep.tile([P, (c1 - c0) * CH], F32, name=name, tag=tag or name, align_bytes=64)
-            if engine == "vector":
+            if engine is nc.vector:
                 nc.vector.tensor_scalar(wg[:], src, gain_sb[:, t : t + 1], None, ALU.mult)
             else:
                 nc.scalar.activation(wg[:], src, ACT.Copy, scale=gain_sb[:, t : t + 1])
             for c in range(c0, c1):
-                wgs[t, c] = (wg, (c - c0) * CH)
+                wg_sb[t, c] = (wg, (c - c0) * CH)
 
         def scatter(t, c0, c1):
-            wg, j0 = wgs[t, c0]
+            wg, j0 = wg_sb[t, c0]
             nc.vector.tensor_tensor(
-                pages[t][:].indirect(idx2[:, c0 * CH // 16 : c1 * CH // 16]),
-                ys[t, c0, c1],
+                pages[t][:].indirect(idx2[:, c0 * CH // PER_COL : c1 * CH // PER_COL]),
+                y_run[t, c0],
                 wg[:, j0 : j0 + (c1 - c0) * CH],
                 ALU.mult,
             )
 
-        def detect_scatter(t, c, side, tag=None):
-            y_tile(t, c, c + 1, tag if HOLD else None)
-            detect(t, c, side)
+        def detect_scatter(t, c, bank_tag, y_tag=None):
+            y_tile(t, c, c + 1, y_tag)
+            detect(t, c, bank_tag)
             scatter(t, c, c + 1)
-
-        out_rows = out_0.rearrange("(p t) m -> p t m", t=PACK)
-
-        def finish_page(t):
-            nc.sync.dma_start(out_rows[:, t, :], pages[t][:])
-            for m0, width, pair in pairs:
-                if TAIL_STYLE == "pairs":
-                    nc.scalar.copy(pair[:, t // 2, :, t % 2], pages[t][:, m0 : m0 + width])
-                else:
-                    pl = pair[:].rearrange("p u m e -> p (u m e)").rearrange("p (t m) -> p t m", t=PACK)
-                    nc.scalar.copy(pl[:, t, :], pages[t][:, m0 : m0 + width])
 
         field_first(0)
         field_first(1)
-        gw1.append(keep.tile([P, S // 2], U32, name="gw1_1", tag="hg0_1_1", align_bytes=64))
-        nc.vector.tensor_copy(gw1[1][:], tw[1][:].indirect(idx[:, 32:64]))
+        got1.append(keep.tile([P, S // 2], U32, name="got1_1", tag="first1_1", align_bytes=64))
+        nc.vector.tensor_copy(got1[1][:], tab[1][:].indirect(idx[:, half_cols : 2 * half_cols]))
         field(1, 0)
         for t in range(PACK):
-            weights("scalar", t, 0)
-        y_tile(2, 1, 4, None)
-        y_tile(3, 1, 4, None)
+            weights(nc.scalar if t < 2 else nc.vector, t, 0)
+        y_tile(2, 1, 4)
+        y_tile(3, 1, 4)
         detect_scatter(0, 0, "zb0")
         detect_scatter(1, 0, "zb1")
         field(1, 1)
-        detect_scatter(2, 0, "zb0", "hplanes1_1")
+        detect_scatter(2, 0, "zb0", "planes1_1")
         detect_scatter(3, 0, "zb1")
         field(2, 0, (0, 1))
         detect_scatter(0, 1, "zb0")
@@ -318,9 +303,9 @@ def tile_list_hologram_detector_page_kernel(
         detect_scatter(1, 1, "zb1")
         field(3, 0, (0, 2))
         detect_scatter(0, 2, "zb0")
-        weights("vector", 1, 2, "hg1_0")
+        weights(nc.vector, 1, 2, "woven1_0")
         field(3, 1)
-        detect_scatter(1, 2, "zb1", "hplanes3_1")
+        detect_scatter(1, 2, "zb1", "planes3_1")
         detect_scatter(0, 3, "zb0")
         detect_scatter(1, 3, "hb1_0")
         detect(2, 1, "hb2_0")
@@ -329,45 +314,37 @@ def tile_list_hologram_detector_page_kernel(
         detect(3, 2, "hb0_1")
         detect(2, 3, "hb1_1")
         detect(3, 3, "zb1")
-        weights("scalar", 2, 1, "hg1_1")
+        weights(nc.scalar, 2, 1, "woven1_1")
         scatter(2, 1, 4)
-        weights("scalar", 3, 1, "hplanes3_1")
+        weights(nc.scalar, 3, 1, "planes3_1")
         scatter(3, 1, 4)
-        pairs = []
-        pair_row = keep.tile([P, PACK * T2], BF16, name="pair_row", tag="wgo1_1")
-        m0 = 0
-        for n, width in enumerate(TAIL):
-            pair = pair_row[:, PACK * m0 : PACK * (m0 + width)].rearrange("p (u m e) -> p u m e", u=2, e=2)
-            pairs.append((m0, width, pair))
-            m0 = m0 + width
-        for t in range(PACK):
-            finish_page(t)
 
-        yscales = keep.tile([P, T2], U8, name="yscales", align_bytes=64)
+        out_rows = out_0.rearrange("(p t) m -> p t m", t=PACK)
+        pair_row = keep.tile([P, PACK * T2], BF16, name="pair_row", tag="wgo1_1")
+        pair = pair_row[:].rearrange("p (u m e) -> p u m e", u=2, e=2)
+        for t in range(PACK):
+            nc.sync.dma_start(out_rows[:, t, :], pages[t][:])
+            if t < PACK - 1:
+                nc.scalar.copy(pair[:, t // 2, :, t % 2], pages[t][:])
+        starts = [sum(TAIL[:n]) for n in range(len(TAIL))]
+        for m0, width in zip(starts, TAIL):
+            nc.scalar.copy(pair[:, 1, m0 : m0 + width, 1], pages[PACK - 1][:, m0 : m0 + width])
+
+        y_scales = keep.tile([P, T2], U8, name="y_scales", align_bytes=64)
         words_out = out_1[0].rearrange("p m t -> p (m t)")
-        for n, (m0, width, pair) in enumerate(pairs):
-            yg = keep.tile([P, width, PACK], BF16, name="yg%d" % n, align_bytes=64)
-            if TAIL_STYLE == "pairs" and n in TAIL_SCALAR:
-                nc.scalar.copy(
-                    yg[:].rearrange("p m t -> p (m t)").bitcast(F32).rearrange("p (m u) -> p m u", u=2),
-                    pair[:].rearrange("p u m e -> p u (m e)").bitcast(F32).rearrange("p u m -> p m u"),
-                )
-            elif TAIL_STYLE == "pairs":
-                nc.vector.tensor_copy(
-                    yg[:].rearrange("p m t -> p (m t)").bitcast(I32).rearrange("p (m u) -> p m u", u=2),
-                    pair[:].rearrange("p u m e -> p u (m e)").bitcast(I32).rearrange("p u m -> p m u"),
-                )
+        for n, (m0, width) in enumerate(zip(starts, TAIL)):
+            y_woven = keep.tile([P, width, PACK], BF16, name="y_woven%d" % n, align_bytes=64)
+            y_flat = y_woven[:].rearrange("p m t -> p (m t)")
+            word = I32 if n < TAIL_ON_VECTOR else F32
+            dst = y_flat.bitcast(word).rearrange("p (m u) -> p m u", u=2)
+            src = pair_row[:].bitcast(word).rearrange("p (u m) -> p m u", u=2)[:, m0 : m0 + width, :]
+            if n < TAIL_ON_VECTOR:
+                nc.vector.tensor_copy(dst, src)
             else:
-                pl = pair[:].rearrange("p u m e -> p (u m e)").rearrange("p (t c i) -> p c t i", t=PACK, i=4)
-                dst = yg[:].rearrange("p (c i) t -> p c t i", i=4)
-                if n in TAIL_SCALAR:
-                    nc.scalar.copy(dst, pl)
-                else:
-                    nc.vector.tensor_copy(dst, pl)
-            ywords = keep.tile([P, width], U32, name="ywords%d" % n, align_bytes=64)
-            nc.vector.quantize_mx(
-                out=ywords[:].bitcast(FP8X4), scales=yscales[:, m0 : m0 + width], in_=yg[:].rearrange("p m t -> p (m t)")
-            )
-            nc.sync.dma_start(words_out[:, 4 * m0 : 4 * (m0 + width)].bitcast(I32), ywords[:].bitcast(I32))
-        for q in range(4):
-            nc.sync.dma_start(out_2[0, 4 * q : 4 * q + 4, :].bitcast(I32), yscales[32 * q : 32 * q + 4, :].bitcast(I32))
+                nc.scalar.copy(dst, src)
+            y_words = keep.tile([P, width], U32, name="y_words%d" % n, align_bytes=64)
+            nc.vector.quantize_mx(out=y_words[:].bitcast(FP8X4), scales=y_scales[:, m0 : m0 + width], in_=y_flat)
+            nc.sync.dma_start(words_out[:, PACK * m0 : PACK * (m0 + width)].bitcast(I32), y_words[:].bitcast(I32))
+        for q in range(QUADS):
+            queue = nc.sync if q < 2 else nc.scalar
+            queue.dma_start(out_2[0, 4 * q : 4 * q + 4, :].bitcast(I32), y_scales[32 * q : 32 * q + 4, :].bitcast(I32))

from contextlib import ExitStack

import concourse.mybir as mybir

K, R, N, T, S, T2 = 1024, 1024, 512, 2048, 1024, 2048
FLOPS = 2 * K * R * S + 2 * R * N * S

F32 = mybir.dt.float32
BF16 = mybir.dt.bfloat16
I32 = mybir.dt.int32
U32 = mybir.dt.uint32
U16 = mybir.dt.uint16
U8 = mybir.dt.uint8
FP8X4 = mybir.dt.float8_e4m3fn_x4
FP4X4 = mybir.dt.float4_e2m1fn_x4
ACT = mybir.ActivationFunctionType
ALU = mybir.AluOpType

P = 128
PACK = 4
QUADS = 4
BLK = P * PACK
CH = 256
HALF = 128
PER_COL = 16
WGO_PARTS = ((0, 0, 1), (1, 0, 1), (0, 1, 2), (0, 2, 4), (1, 1, 4))
SHORT, LONG = 256, 512
TAIL = (SHORT, SHORT, LONG, LONG, SHORT, SHORT)
TAIL_ON_VECTOR = 4


def tile_list_hologram_detector_page_kernel(
    tc, tab_words, tab_scales, offs, pc, ps, ref, wd_words, wd_scales, gain, wgo, offs2, out_0, out_1, out_2
):
    nc = tc.nc
    with ExitStack() as ctx:
        keep = ctx.enter_context(tc.tile_pool(name="keep", bufs=1))
        psum = ctx.enter_context(tc.psum_pool(name="psum", bufs=1))

        idx = keep.tile([P, S // PER_COL], U16, name="idx")
        idx2 = keep.tile([P, S // PER_COL], U16, name="idx2")
        nc.sync.dma_start(idx[:], offs)

        tab_sc = keep.tile([P, T], U8, name="tab_sc", tag="pc0_codes", align_bytes=64)
        wd_sc_raw = keep.tile([P, 2, N], U8, name="wd_sc_raw", align_bytes=64)
        nc.gpsimd.memset(tab_sc[:].bitcast(I32), 0)
        nc.gpsimd.memset(wd_sc_raw[:].bitcast(I32), 0)

        def load_cols(src, part, name, tag=None):
            raw = keep.tile([P, PACK, CH], F32, name=name, tag=tag or name, align_bytes=64)
            nc.sync.dma_start(raw[:], src.rearrange("(p i) r -> p i r", i=PACK)[:, :, part * CH : (part + 1) * CH])
            return raw

        def load_table(a, pieces):
            tile = keep.tile([P, T], U32, name="tab%d" % a, align_bytes=64)
            words = tab_words[a].rearrange("p n t -> p (n t)").bitcast(I32)
            width = T // pieces
            for h in range(pieces):
                cols = slice(h * width, (h + 1) * width)
                nc.sync.dma_start(tile[:, cols].bitcast(I32), words[:, cols])
            return tile

        ref_sb = keep.tile([P, 2, PACK], F32, name="ref_sb")
        gain_sb = keep.tile([P, PACK], F32, name="gain_sb")
        wd_raw = keep.tile([P, 2, 2 * N], U8, name="wd_raw", align_bytes=64)
        nc.sync.dma_start(idx2[:], offs2)
        tab = [load_table(0, 2)]
        for a in range(2):
            nc.sync.dma_start(wd_raw[:, a, :].bitcast(I32), wd_words[a].bitcast(I32))
        nc.sync.dma_start(ref_sb[:], ref.rearrange("(b p t) -> p b t", b=2, t=PACK))
        pc_raw = [load_cols(pc, 0, "pc_raw0", "page2")]
        for q in range(QUADS):
            nc.sync.dma_start(
                tab_sc[32 * q : 32 * q + 8, :].bitcast(I32), tab_scales[:, 4 * q : 4 * q + 4, :].bitcast(I32)
            )
        pc_raw.append(load_cols(pc, 1, "pc_raw1", "page3"))
        ps_raw = [load_cols(ps, part, "ps_raw%d" % part) for part in range(2)]
        tab.append(load_table(1, 1))
        pc_raw.extend(load_cols(pc, part, "pc_raw%d" % part) for part in range(2, 4))
        ps_raw.append(load_cols(ps, 2, "ps_raw2", "planes1_0"))
        ps_raw.append(load_cols(ps, 3, "ps_raw3"))
        for q in range(QUADS):
            nc.sync.dma_start(
                wd_sc_raw[32 * q : 32 * q + 4, :, :].bitcast(I32),
                wd_scales[:, 4 * q : 4 * q + 4, :].rearrange("a r n -> r a n").bitcast(I32),
            )
        nc.sync.dma_start(gain_sb[:], gain.rearrange("(p t) -> p t", t=PACK))

        wgo_rows = wgo.rearrange("(q t) j -> q t j", t=PACK)
        wgo_sb = {}
        for u, c0, c1 in WGO_PARTS:
            name = "wgo%d_%d" % (u, c0)
            part_tile = keep.tile([P, 2, (c1 - c0) * CH], F32, name=name, tag=name)
            for q in (0, 2, 1, 3):
                nc.sync.dma_start(
                    part_tile[32 * q : 32 * q + 32, :, :], wgo_rows[:, 2 * u : 2 * u + 2, c0 * CH : c1 * CH]
                )
            for e in range(2):
                wgo_sb[2 * u + e, c0] = (part_tile[:, e, :], c1)

        pages = []
        for t in range(2):
            page = keep.tile([P, T2], F32, name="page%d" % t)
            for h in range(2):
                nc.vector.memset(page[:, h * T2 // 2 : (h + 1) * T2 // 2], 0.0)
            pages.append(page)

        got_sc = keep.tile([P, S], U8, name="got_sc", align_bytes=64)
        got0 = keep.tile([P, S], U32, name="got0", align_bytes=64)
        got1 = [keep.tile([P, S // 2], U32, name="got1_0", align_bytes=64)]

        def gathered(a, j0, width):
            if a == 0:
                return got0[:, j0 : j0 + width]
            half, j = divmod(j0, S // 2)
            return got1[half][:, j : j + width]

        def deal_views(grouped, raw, half):
            m = CH // PACK
            dst = grouped[:, :, half * m : (half + 1) * m, :].rearrange("p t m i -> p m t i")
            return dst, raw[:].rearrange("p i (m t) -> p m t i", t=PACK)

        def deal_scalar(grouped, raw, half, sign):
            dst, src = deal_views(grouped, raw, half)
            nc.scalar.activation(dst, src, ACT.Copy, scale=sign)

        def quantise(src, width, name, codes_tag=None):
            codes = keep.tile([P, width], U32, name=name + "_codes", tag=codes_tag or name + "_codes", align_bytes=64)
            scales = keep.tile([P, width], U8, name=name + "_scales", align_bytes=64)
            nc.vector.quantize_mx(out=codes[:].bitcast(FP8X4), scales=scales[:], in_=src)
            return codes, scales

        def new_grouped(name):
            return keep.tile([P, PACK, P, PACK], BF16, name=name, tag=name, align_bytes=64)

        def flat(grouped):
            return grouped[:].rearrange("p t m i -> p (t m i)")

        wd = keep.tile([P, 2, PACK, P, 2], U8, name="wd", align_bytes=64)
        for a in range(2):
            nc.vector.tensor_copy(
                wd[:, a].rearrange("p t m e -> p (t m e)").bitcast(U16).rearrange("p (t m) -> p m t", t=PACK),
                wd_raw[:, a, :].bitcast(U16).rearrange("p (m t) -> p m t", t=PACK),
            )

        prop = {}
        grouped = new_grouped("pc0_bf16")
        for half in range(2):
            deal_scalar(grouped, pc_raw[half], half, 1.0)
        for t in range(2, PACK):
            page = keep.tile([P, T2], F32, name="page%d" % t, tag="page%d" % t, align_bytes=64)
            for c0 in range(0, T2, CH):
                nc.gpsimd.memset(page[:, c0 : c0 + CH], 0.0)
            pages.append(page)
        nc.vector.tensor_copy(got0[:], tab[0][:].indirect(idx[:]))
        nc.vector.tensor_copy(got_sc[:], tab_sc[:].indirect(idx[:]))
        prop[0, 0] = quantise(flat(grouped), BLK, "pc0")
        grouped = new_grouped("ps0_bf16")
        for half in range(2):
            deal_scalar(grouped, ps_raw[half], half, -1.0)
        prop[1, 0] = quantise(flat(grouped), BLK, "ps0")
        half_cols = S // 2 // PER_COL
        nc.vector.tensor_copy(got1[0][:], tab[1][:].indirect(idx[:, 0:half_cols]))
        grouped = new_grouped("pc1_bf16")
        for half in range(2):
            deal_scalar(grouped, pc_raw[2 + half], half, 1.0)
        prop[0, 1] = quantise(flat(grouped), BLK, "pc1", "ps0_bf16")
        grouped = new_grouped("ps1_bf16")
        deal_scalar(grouped, ps_raw[2], 0, -1.0)
        dst, src = deal_views(grouped, ps_raw[3], 1)
        nc.vector.tensor_scalar(dst, src, -1.0, None, ALU.mult)
        prop[1, 1] = quantise(flat(grouped), BLK, "ps1")
        wd_sc = keep.tile([P, 2, PACK, P], U8, name="wd_sc", tag="ps1_bf16", align_bytes=64)
        nc.vector.tensor_copy(
            wd_sc[:].rearrange("p a t m -> p a m t"), wd_sc_raw[:].rearrange("p a (m t) -> p a m t", t=PACK)
        )

        def field_pass(out, a, b, t, j0, width, start, stop):
            codes, scales = prop[a, b]
            nc.tensor.matmul_mx(
                out=out,
                lhsT=codes[:, t * P : (t + 1) * P].bitcast(FP8X4),
                lhsT_scale=scales[:, t * P : (t + 1) * P],
                rhs=gathered(a, j0, width).bitcast(FP8X4),
                rhs_scale=got_sc[4 * a : P, j0 : j0 + width],
                start=start,
                stop=stop,
            )

        h_mx = {}

        def field_first(b):
            banks = [psum.tile([P, PACK, HALF], F32, name="h_bank", tag="hb%d_%d" % (b, jh)) for jh in range(2)]
            for a in range(2):
                for jh in range(2):
                    for t in range(PACK):
                        first, last = a == 0 and t == 0, a == 1 and t == PACK - 1
                        field_pass(banks[jh][:, t, :], a, b, t, jh * HALF, HALF, first, last)
            woven = []
            for jh in range(2):
                name = "first%d_%d" % (b, jh)
                tile = keep.tile([P, HALF, PACK], BF16, name=name, tag=name, align_bytes=64)
                nc.vector.tensor_tensor(
                    tile[:],
                    banks[jh][:].rearrange("p t j -> p j t"),
                    ref_sb[:, b : b + 1, :].to_broadcast([P, HALF, PACK]),
                    ALU.add,
                )
                woven.append(tile)
            for jh in range(2):
                codes, scales = quantise(woven[jh][:].rearrange("p j t -> p (j t)"), HALF, "h0_%d_%d" % (b, jh))
                h_mx[0, b, jh] = (codes[:], scales[:])

        def field(c, b, weight_part=None):
            planes_tag = "planes%d_%d" % (c, b)
            planes = keep.tile([P, PACK, CH], BF16, name="planes", tag=planes_tag, align_bytes=64)
            for u in range(2):
                bank = psum.tile([P, 2, CH], F32, name="h_bank", tag="hb%d_%d" % ((2 * c + b) % 3, u))
                for e in range(2):
                    for a in range(2):
                        field_pass(bank[:, e, :], a, b, 2 * u + e, c * CH, CH, a == 0, a == 1)
                for e in range(2):
                    t = 2 * u + e
                    nc.scalar.activation(planes[:, t, :], bank[:, e, :], ACT.Identity, bias=ref_sb[:, b, t : t + 1])
            woven = keep.tile([P, CH, PACK], BF16, name="woven", tag="woven%d_%d" % (c % 2, b), align_bytes=64)
            nc.scalar.copy(
                woven[:].rearrange("p (c i) t -> p c t i", i=4), planes[:].rearrange("p t (c i) -> p c t i", i=4)
            )
            if weight_part is not None:
                weights(nc.vector, weight_part[0], weight_part[1], planes_tag)
            codes, scales = quantise(woven[:].rearrange("p j t -> p (j t)"), CH, "h%d_%d" % (c, b))
            for jh in range(2):
                cols = slice(jh * HALF, (jh + 1) * HALF)
                h_mx[c, b, jh] = (codes[:, cols], scales[:, cols])

        y_chunk, y_run, wg_sb = {}, {}, {}

        def y_tile(t, c0, c1, tag=None):
            name = "y%d_%d" % (t, c0)
            y = keep.tile([P, (c1 - c0) * CH], F32, name=name, tag=tag or name, align_bytes=64)
            for c in range(c0, c1):
                y_chunk[t, c] = y[:, (c - c0) * CH : (c - c0 + 1) * CH]
            y_run[t, c0] = y[:]

        def detect(t, c, bank_tag):
            bank = psum.tile([P, CH], F32, name="z_bank", tag=bank_tag)
            for jh in range(2):
                for b in range(2):
                    codes, scales = h_mx[c, b, jh]
                    nc.tensor.matmul_mx(
                        out=bank[:, jh * HALF : (jh + 1) * HALF],
                        lhsT=wd[:, b, t].rearrange("p m e -> p (m e)").bitcast(FP4X4),
                        lhsT_scale=wd_sc[:, b, t, :],
                        rhs=codes.bitcast(FP8X4),
                        rhs_scale=scales,
                        start=(b == 0),
                        stop=(b == 1),
                    )
            nc.scalar.activation(y_chunk[t, c], bank[:], ACT.Tanh)

        def weights(engine, t, c0, tag=None):
            src, c1 = wgo_sb[t, c0]
            name = "wg%d_%d" % (t, c0)
            wg = keep.tile([P, (c1 - c0) * CH], F32, name=name, tag=tag or name, align_bytes=64)
            if engine is nc.vector:
                nc.vector.tensor_scalar(wg[:], src, gain_sb[:, t : t + 1], None, ALU.mult)
            else:
                nc.scalar.activation(wg[:], src, ACT.Copy, scale=gain_sb[:, t : t + 1])
            for c in range(c0, c1):
                wg_sb[t, c] = (wg, (c - c0) * CH)

        def scatter(t, c0, c1):
            wg, j0 = wg_sb[t, c0]
            nc.vector.tensor_tensor(
                pages[t][:].indirect(idx2[:, c0 * CH // PER_COL : c1 * CH // PER_COL]),
                y_run[t, c0],
                wg[:, j0 : j0 + (c1 - c0) * CH],
                ALU.mult,
            )

        def detect_scatter(t, c, bank_tag, y_tag=None):
            y_tile(t, c, c + 1, y_tag)
            detect(t, c, bank_tag)
            scatter(t, c, c + 1)

        field_first(0)
        field_first(1)
        got1.append(keep.tile([P, S // 2], U32, name="got1_1", tag="first1_1", align_bytes=64))
        nc.vector.tensor_copy(got1[1][:], tab[1][:].indirect(idx[:, half_cols : 2 * half_cols]))
        field(1, 0)
        for t in range(PACK):
            weights(nc.scalar if t < 2 else nc.vector, t, 0)
        y_tile(2, 1, 4)
        y_tile(3, 1, 4)
        detect_scatter(0, 0, "zb0")
        detect_scatter(1, 0, "zb1")
        field(1, 1)
        detect_scatter(2, 0, "zb0", "planes1_1")
        detect_scatter(3, 0, "zb1")
        field(2, 0, (0, 1))
        detect_scatter(0, 1, "zb0")
        field(2, 1, (1, 1))
        detect_scatter(1, 1, "zb1")
        field(3, 0, (0, 2))
        detect_scatter(0, 2, "zb0")
        weights(nc.vector, 1, 2, "woven1_0")
        field(3, 1)
        detect_scatter(1, 2, "zb1", "planes3_1")
        detect_scatter(0, 3, "zb0")
        detect_scatter(1, 3, "hb1_0")
        detect(2, 1, "hb2_0")
        detect(3, 1, "hb2_1")
        detect(2, 2, "hb0_0")
        detect(3, 2, "hb0_1")
        detect(2, 3, "hb1_1")
        detect(3, 3, "zb1")
        weights(nc.scalar, 2, 1, "woven1_1")
        scatter(2, 1, 4)
        weights(nc.scalar, 3, 1, "planes3_1")
        scatter(3, 1, 4)

        out_rows = out_0.rearrange("(p t) m -> p t m", t=PACK)
        pair_row = keep.tile([P, PACK * T2], BF16, name="pair_row", tag="wgo1_1")
        pair = pair_row[:].rearrange("p (u m e) -> p u m e", u=2, e=2)
        for t in range(PACK):
            nc.sync.dma_start(out_rows[:, t, :], pages[t][:])
            if t < PACK - 1:
                nc.scalar.copy(pair[:, t // 2, :, t % 2], pages[t][:])
        starts = [sum(TAIL[:n]) for n in range(len(TAIL))]
        for m0, width in zip(starts, TAIL):
            nc.scalar.copy(pair[:, 1, m0 : m0 + width, 1], pages[PACK - 1][:, m0 : m0 + width])

        y_scales = keep.tile([P, T2], U8, name="y_scales", align_bytes=64)
        words_out = out_1[0].rearrange("p m t -> p (m t)")
        for n, (m0, width) in enumerate(zip(starts, TAIL)):
            y_woven = keep.tile([P, width, PACK], BF16, name="y_woven%d" % n, align_bytes=64)
            y_flat = y_woven[:].rearrange("p m t -> p (m t)")
            word = I32 if n < TAIL_ON_VECTOR else F32
            dst = y_flat.bitcast(word).rearrange("p (m u) -> p m u", u=2)
            src = pair_row[:].bitcast(word).rearrange("p (u m) -> p m u", u=2)[:, m0 : m0 + width, :]
            if n < TAIL_ON_VECTOR:
                nc.vector.tensor_copy(dst, src)
            else:
                nc.scalar.copy(dst, src)
            y_words = keep.tile([P, width], U32, name="y_words%d" % n, align_bytes=64)
            nc.vector.quantize_mx(out=y_words[:].bitcast(FP8X4), scales=y_scales[:, m0 : m0 + width], in_=y_flat)
            nc.sync.dma_start(words_out[:, PACK * m0 : PACK * (m0 + width)].bitcast(I32), y_words[:].bitcast(I32))
        for q in range(QUADS):
            queue = nc.sync if q < 2 else nc.scalar
            queue.dma_start(out_2[0, 4 * q : 4 * q + 4, :].bitcast(I32), y_scales[32 * q : 32 * q + 4, :].bitcast(I32))
